import numpy as np
import ml_dtypes


def mxq(x, axis, fmt="e4m3"):
    dtype, down = {"e4m3": (ml_dtypes.float8_e4m3fn, 7), "e5m2": (ml_dtypes.float8_e5m2, 14)}[fmt]
    v = np.moveaxis(np.asarray(x, np.float32).astype(ml_dtypes.bfloat16).astype(np.float64), axis, -1)
    blocks = v.reshape(v.shape[:-1] + (-1, 32))
    amax = np.abs(blocks).max(-1, keepdims=True)
    byte = np.maximum(np.where(amax > 0, np.frexp(amax)[1] - 1 + 127, 0) - down, 1)
    scale = np.exp2(byte - 127.0)
    codes = (blocks / scale).astype(np.float32).astype(dtype).astype(np.float64)
    return np.moveaxis((codes * scale).reshape(v.shape), -1, axis)


WIDE = False


def mx_kscale(k):
    if not WIDE:
        return np.ones(k)
    levels = np.array([10, -10, 5, -5, 0])
    if k % 512:
        return np.exp2(np.random.permutation(np.resize(levels, k // 32))).repeat(32)
    a = np.empty((k // 512, 16))
    for p in range(k // 512):
        a[p, :8] = np.random.permutation(np.resize(levels, 8))
        for g in range(8):
            far = levels[np.abs(levels - a[p, g]) >= 10]
            a[p, g + 8] = far[np.random.randint(len(far))]
    return np.exp2(a.ravel()).repeat(32)


def f64(x):
    return np.asarray(x).astype(np.float64)


def striped(idx):
    return np.tile(idx.reshape(-1, 16).T, (8, 1)).astype(np.uint16)


def unstriped(offs):
    return offs[:16].T.reshape(-1).astype(np.int64)


E2M1 = np.array([0.0, 0.5, 1.0, 1.5, 2.0, 3.0, 4.0, 6.0, -0.0, -0.5, -1.0, -1.5, -2.0, -3.0, -4.0, -6.0])


def pack_weight(w, fmt):
    k, n = w.shape
    w = f64(np.asarray(w, np.float32).astype(ml_dtypes.bfloat16)).reshape(k // 32, 32, n)
    amax = np.abs(w).max(1)
    if fmt == "e4m3":
        byte = np.frexp(amax)[1] - 1 + 127 - 7
    else:
        mant, ex = np.frexp(amax / 6.0)
        byte = np.where(mant > 0.5, ex, ex - 1) + 127
    byte = np.clip(np.where(amax > 0, byte, 1), 1, 254)
    scaled = (w * np.exp2(127.0 - byte)[:, None, :]).reshape(k, n).astype(np.float32)
    by_word = np.ascontiguousarray(scaled.reshape(k // 512, 128, 4, n).transpose(0, 1, 3, 2))
    if fmt == "e4m3":
        words = by_word.astype(ml_dtypes.float8_e4m3fn).view(np.uint8)
    else:
        c = by_word.astype(ml_dtypes.float4_e2m1fn).view(np.uint8) & 0xF
        words = (c[..., 0::2] | (c[..., 1::2] << 4)).reshape(k // 512, 128, 2 * n)
    return np.ascontiguousarray(words), np.ascontiguousarray(byte.astype(np.uint8).reshape(k // 512, 16, n))


def unpack_weight(words, scales, fmt):
    g, _, n = scales.shape
    words = np.ascontiguousarray(words).reshape(g, 128, n, -1)
    if fmt == "e4m3":
        vals = words.view(ml_dtypes.float8_e4m3fn).astype(np.float64)
    else:
        nib = np.empty((g, 128, n, 4), np.uint8)
        nib[..., 0::2] = words & 0xF
        nib[..., 1::2] = words >> 4
        vals = E2M1[nib]
    vals = vals * np.repeat(np.exp2(scales.astype(np.float64) - 127.0), 8, axis=1)[..., None]
    return vals.transpose(0, 1, 3, 2).reshape(g * 512, n)


def gelu(v):
    return 0.5 * v * (1.0 + np.tanh(np.sqrt(2.0 / np.pi) * (v + 0.044715 * v**3)))


def bf(x):
    return np.asarray(x, np.float32).astype(ml_dtypes.bfloat16)

def planes(Y):
    n, m = Y.shape
    b = f64(bf(Y)).reshape(n // 32, 32, m)
    amax = np.abs(b).max(1)
    byte = np.clip(np.where(amax > 0, np.frexp(amax)[1] - 1 + 127 - 7, 1), 1, 254)
    codes = (b * np.exp2(127.0 - byte)[:, None, :]).reshape(n, m).astype(np.float32).astype(ml_dtypes.float8_e4m3fn).view(np.uint8)
    words = codes.reshape(n // 512, 128, 4, m).transpose(0, 1, 3, 2)
    return np.ascontiguousarray(words), np.ascontiguousarray(byte.astype(np.uint8).reshape(n // 512, 16, m))


K, T, S, H, N = 1024, 4096, 1024, 512, 512

def setup_inputs():
    n = np.random.standard_normal
    s = mx_kscale(K)[:, None]
    u = mx_kscale(H)[:, None]
    tab_words, tab_scales = pack_weight(n((K, T)) * s, "e4m3")
    offs = striped(np.random.permutation(T)[:S])
    we = (n((K, H)) / np.sqrt(K) / s).astype(np.float32)
    g = (np.exp(0.3 * n(H)) * u[:, 0]).astype(np.float32)
    m = np.exp(1.5 * n((H, N)))
    m = m / m.sum(axis=0, keepdims=True)
    wm_words, wm_scales = pack_weight(m / u, "e4m3")
    wp_words, wp_scales = pack_weight(n((K, N)) / np.sqrt(K) / s, "e2m1")
    gain = np.exp(0.8 * n(N)).astype(np.float32)
    return {"tab_words": tab_words, "tab_scales": tab_scales, "offs": offs, "we": we, "g": g,
            "wm_words": wm_words, "wm_scales": wm_scales,
            "wp_words": wp_words, "wp_scales": wp_scales, "gain": gain}

def reference(tab_words, tab_scales, offs, we, g, wm_words, wm_scales, wp_words, wp_scales, gain):
    v = unpack_weight(tab_words, tab_scales, "e4m3")[:, unstriped(offs)]
    wm = unpack_weight(wm_words, wm_scales, "e4m3")
    wp = unpack_weight(wp_words, wp_scales, "e2m1")
    leaf = f64(g)[:, None] * np.exp(mxq(f64(we), 0, "e4m3").T @ v)
    mix = wm.T @ mxq(leaf, 0, "e4m3")
    prior = wp.T @ v
    y = f64(gain)[:, None] * (np.log(mix) + prior)
    words, scales = planes(y)
    return y, words, scales

@@ -1,0 +1,235 @@
+from contextlib import ExitStack
+
+import concourse.mybir as mybir
+
+K, T, S, H, N = 1024, 4096, 1024, 512, 512
+FLOPS = 2 * S * (K * H + H * N + K * N)
+
+F32 = mybir.dt.float32
+BF16 = mybir.dt.bfloat16
+I32 = mybir.dt.int32
+U32 = mybir.dt.uint32
+U16 = mybir.dt.uint16
+U8 = mybir.dt.uint8
+FP8X4 = mybir.dt.float8_e4m3fn_x4
+FP4X4 = mybir.dt.float4_e2m1fn_x4
+ACT = mybir.ActivationFunctionType
+ALU = mybir.AluOpType
+
+P = 128
+PACK = 4
+PASSES = 2
+HALF = 512
+HALVES = 2
+QUARTER = 256
+
+
+def interleave(copy, dst, src):
+    copy(out=dst.rearrange("p (c i) t -> p c t i", i=4), in_=src.rearrange("p t (c i) -> p c t i", i=4))
+
+
+def tile_list_stroke_circuit_evidence_kernel(
+    tc, tab_words, tab_scales, offs, we, g, wm_words, wm_scales, wp_words, wp_scales, gain, out_0, out_1, out_2
+):
+    nc = tc.nc
+    with ExitStack() as ctx:
+        keep = ctx.enter_context(tc.tile_pool(name="keep", bufs=1))
+        psum = ctx.enter_context(tc.psum_pool(name="psum", bufs=1))
+
+        def sb(name, shape, dtype, tag=None):
+            return keep.tile(shape, dtype, name=name, tag=tag or name, align_bytes=64)
+
+        def bank(b):
+            return psum.tile([P, HALF], F32, name="bank%d" % b)
+
+        offsets = keep.tile([P, S // 16], U16, name="offsets")
+        nc.sync.dma_start(offsets[:], offs)
+
+        tab_sc = sb("tab_sc", [P, T], U8, tag="first")
+        nc.vector.memset(tab_sc[:].bitcast(I32), 0)
+        w_sc_raw = sb("w_sc_raw", [P, PASSES, N], U8)
+        nc.vector.memset(w_sc_raw[:].bitcast(I32), 0)
+        v_sc1 = sb("v_sc1", [P, S], U8)
+        nc.vector.memset(v_sc1[:].bitcast(I32), 0)
+
+        wp_raw = sb("wp_raw", [P, PASSES, 2 * N], U8, tag="third")
+        nc.sync.dma_start(wp_raw[:].bitcast(I32), wp_words.rearrange("a p c -> p a c").bitcast(I32))
+        tab0 = sb("tab0", [P, T], I32, tag="second")
+        nc.sync.dma_start(tab0[:], tab_words[0].rearrange("p c i -> p (c i)").bitcast(I32))
+        g_sb = sb("g_sb", [P, PACK], F32)
+        nc.scalar.dma_start(g_sb[:], g.rearrange("(p t) -> p t", t=PACK))
+        gain_sb = sb("gain_sb", [P, PACK], F32)
+        nc.scalar.dma_start(gain_sb[:], gain.rearrange("(p t) -> p t", t=PACK))
+        for q in range(4):
+            nc.scalar.dma_start(
+                tab_sc[32 * q : 32 * q + 8, :].bitcast(I32), tab_scales[:, 4 * q : 4 * q + 4, :].bitcast(I32)
+            )
+        for q in range(4):
+            nc.scalar.dma_start(
+                w_sc_raw[32 * q : 32 * q + 4, :, :].bitcast(I32),
+                wp_scales[:, 4 * q : 4 * q + 4, :].rearrange("a r n -> r a n").bitcast(I32),
+            )
+
+        log_g = sb("log_g", [P, PACK], F32)
+        nc.scalar.activation(log_g[:], g_sb[:], ACT.Ln)
+        warm = sb("warm", [P, PACK], F32)
+        nc.scalar.activation(warm[:], log_g[:], ACT.Exp)
+
+        wp = sb("wp", [P, PASSES, 2 * N], U8)
+        nc.vector.tensor_copy(
+            out=wp[:].bitcast(U16).rearrange("p a (t c i) -> p a c t i", t=PACK, i=8),
+            in_=wp_raw[:].bitcast(U16).rearrange("p a (c i t) -> p a c t i", t=PACK, i=8),
+        )
+        tab1 = sb("tab1", [P, T], I32, tag="third")
+        nc.sync.dma_start(tab1[:], tab_words[1].rearrange("p c i -> p (c i)").bitcast(I32))
+
+        v_sc = sb("v_sc", [P, S], U8)
+        nc.vector.tensor_copy(v_sc[:], tab_sc[:].indirect(offsets[:]))
+        nc.scalar.dma_start(v_sc1[0:112, :].bitcast(I32), v_sc[4:116, :].bitcast(I32))
+        we_raw = [sb("we_raw0", [P, PACK, H], F32, tag="first")]
+        nc.sync.dma_start(we_raw[0][:], we[0:512, :].rearrange("(p j) r -> p j r", j=PACK))
+
+        v0 = sb("v0", [P, S], U32)
+        nc.vector.tensor_copy(v0[:], tab0[:].bitcast(U32).indirect(offsets[:]))
+        we_raw.append(sb("we_raw1", [P, PACK, H], F32, tag="second"))
+        nc.sync.dma_start(we_raw[1][:], we[512:1024, :].rearrange("(p j) r -> p j r", j=PACK))
+
+        wp_sc = sb("wp_sc", [P, PASSES, N], U8)
+        nc.vector.tensor_copy(
+            out=wp_sc[:].rearrange("p a (t c i) -> p a c t i", t=PACK, i=16),
+            in_=w_sc_raw[:].rearrange("p a (c i t) -> p a c t i", t=PACK, i=16),
+        )
+        wm_sc_raw = w_sc_raw[:, 0, :]
+        for q in range(4):
+            nc.sync.dma_start(
+                w_sc_raw[32 * q : 32 * q + 4, 0, :].bitcast(I32), wm_scales[0, 4 * q : 4 * q + 4, :].bitcast(I32)
+            )
+        v1 = [sb("v1_%d" % h, [P, HALF], U32) for h in range(HALVES)]
+        for h in range(HALVES):
+            nc.vector.tensor_copy(v1[h][:], tab1[:].bitcast(U32).indirect(offsets[:, 32 * h : 32 * (h + 1)]))
+        wm_raw = sb("wm_raw", [P, N], I32, tag="third")
+        nc.sync.dma_start(wm_raw[:], wm_words[0].rearrange("p c i -> p (c i)").bitcast(I32))
+
+        def v_words(a, h):
+            return (v0[:, HALF * h : HALF * (h + 1)] if a == 0 else v1[h][:]).bitcast(FP8X4)
+
+        acc = [[bank(PACK * h + t) for t in range(PACK)] for h in range(HALVES)]
+        for a in range(PASSES):
+            for h in range(HALVES):
+                for t in range(PACK):
+                    nc.tensor.matmul_mx(
+                        acc[h][t][:],
+                        lhsT=wp[:, a, 2 * P * t : 2 * P * (t + 1)].bitcast(FP4X4),
+                        lhsT_scale=wp_sc[:, a, P * t : P * (t + 1)],
+                        rhs=v_words(a, h),
+                        rhs_scale=(v_sc if a == 0 else v_sc1)[:, HALF * h : HALF * (h + 1)],
+                        start=(a == 0),
+                        stop=(a == PASSES - 1),
+                    )
+        prior = [[sb("prior%d_%d" % (h, t), [P, HALF], F32) for t in range(PACK)] for h in range(HALVES)]
+        for h in range(HALVES):
+            for t in range(PACK):
+                nc.scalar.activation(prior[h][t][:], acc[h][t][:], ACT.Copy, scale=gain_sb[:, t : t + 1])
+
+        we_q = {}
+        for a in range(PASSES):
+            for u in range(2):
+                grouped = sb("we_g%d_%d" % (a, u), [P, 2, P, PACK], BF16)
+                nc.vector.tensor_copy(
+                    out=grouped[:].rearrange("p t m j -> p m t j"),
+                    in_=we_raw[a][:].rearrange("p j (m t) -> p m t j", t=PACK)[:, :, 2 * u : 2 * u + 2, :],
+                )
+                codes = sb("we_c%d_%d" % (a, u), [P, 2 * P], U32)
+                scales = sb("we_s%d_%d" % (a, u), [P, 2 * P], U8)
+                nc.vector.quantize_mx(
+                    out=codes[:].bitcast(FP8X4), scales=scales[:], in_=grouped[:].rearrange("p t m j -> p (t m j)")
+                )
+                we_q[a, u] = (codes, scales)
+
+        wm = sb("wm", [P, N], I32)
+        nc.vector.tensor_copy(
+            out=wm[:].rearrange("p (t c i) -> p c t i", t=PACK, i=4),
+            in_=wm_raw[:].rearrange("p (c i t) -> p c t i", t=PACK, i=4),
+        )
+        wm_sc = sb("wm_sc", [P, N], U8)
+        nc.vector.tensor_copy(
+            out=wm_sc[:].rearrange("p (t c i) -> p c t i", t=PACK, i=16),
+            in_=wm_sc_raw.rearrange("p (c i t) -> p c t i", t=PACK, i=16),
+        )
+
+        acc = [[bank(PACK * h + t) for t in range(PACK)] for h in range(HALVES)]
+        for h in range(HALVES):
+            for a in range(PASSES):
+                for t in range(PACK):
+                    codes, scales = we_q[a, t // 2]
+                    cols = slice(P * (t % 2), P * (t % 2 + 1))
+                    nc.tensor.matmul_mx(
+                        acc[h][t][:],
+                        lhsT=codes[:, cols].bitcast(FP8X4),
+                        lhsT_scale=scales[:, cols],
+                        rhs=v_words(a, h),
+                        rhs_scale=v_sc[4 * a : P, HALF * h : HALF * (h + 1)],
+                        start=(a == 0),
+                        stop=(a == PASSES - 1),
+                    )
+        leaf_q = []
+        for h in range(HALVES):
+            rows = sb("leaf_rows%d" % h, [P, PACK, HALF], BF16)
+            for t in range(PACK):
+                nc.scalar.activation(rows[:, t, :], acc[h][t][:], ACT.Exp, bias=log_g[:, t : t + 1])
+            grouped = sb("leaf_g%d" % h, [P, HALF, PACK], BF16)
+            interleave(nc.vector.tensor_copy, grouped[:], rows[:])
+            codes = sb("leaf_c%d" % h, [P, HALF], U32)
+            scales = sb("leaf_s%d" % h, [P, HALF], U8)
+            nc.vector.quantize_mx(
+                out=codes[:].bitcast(FP8X4), scales=scales[:], in_=grouped[:].rearrange("p j t -> p (j t)")
+            )
+            leaf_q.append((codes, scales))
+
+        clock = sb("clock", [P, 16], F32)
+        nc.gpsimd.tensor_copy(clock[:, 0:1], prior[1][3][:, 0:1])
+        nc.gpsimd.tensor_copy(clock[:, 8:9], rows[:, 3, 0:1])
+        out_rows = out_0.rearrange("(p t) j -> p t j", t=PACK)
+        y = []
+        for h in range(HALVES):
+            y.append(sb("y%d" % h, [P, PACK, HALF], F32))
+            for t in range(PACK):
+                mix = bank(7 - t if h == 0 else t)
+                nc.tensor.matmul_mx(
+                    mix[:],
+                    lhsT=wm[:, P * t : P * (t + 1)].bitcast(FP8X4),
+                    lhsT_scale=wm_sc[:, P * t : P * (t + 1)],
+                    rhs=leaf_q[h][0][:].bitcast(FP8X4),
+                    rhs_scale=leaf_q[h][1][:],
+                    start=True,
+                    stop=True,
+                )
+                log_mix = sb("log_mix%d_%d" % (h, t), [P, HALF], F32)
+                nc.scalar.activation(log_mix[:], mix[:], ACT.Ln)
+                nc.vector.scalar_tensor_tensor(
+                    y[h][:, t, :], log_mix[:], gain_sb[:, t : t + 1], prior[h][t][:], ALU.mult, ALU.add
+                )
+                if t % 2 == 1:
+                    nc.sync.dma_start(
+                        out_rows[:, t - 1 : t + 1, HALF * h : HALF * (h + 1)], y[h][:, t - 1 : t + 1, :]
+                    )
+
+        out_words = out_1[0].rearrange("p m t -> p (m t)").bitcast(I32)
+        y_sc = sb("y_sc", [P, S], U8)
+        for name, copy, h, lo, width in (
+            ("a", nc.scalar.copy, 0, 0, QUARTER),
+            ("b", nc.vector.tensor_copy, 1, 0, HALF),
+            ("c", nc.scalar.copy, 0, QUARTER, QUARTER),
+        ):
+            grouped = sb("y_g" + name, [P, width, PACK], BF16)
+            interleave(copy, grouped[:], y[h][:, :, lo : lo + width])
+            codes = sb("y_c" + name, [P, width], I32)
+            cols = slice(HALF * h + lo, HALF * h + lo + width)
+            nc.vector.quantize_mx(
+                out=codes[:].bitcast(FP8X4), scales=y_sc[:, cols], in_=grouped[:].rearrange("p j t -> p (j t)")
+            )
+            nc.sync.dma_start(out_words[:, cols], codes[:])
+        for q in range(4):
+            (nc.sync if q % 2 == 0 else nc.scalar).dma_start(
+                out_2[0, 4 * q : 4 * q + 4, :].bitcast(I32), y_sc[32 * q : 32 * q + 4, :].bitcast(I32)
+            )

@@ -22,6 +22,7 @@ PASSES = 2
 HALF = 512
 HALVES = 2
 QUARTER = 256
+LEAD = 1024
 
 
 def interleave(copy, dst, src):
@@ -45,30 +46,34 @@ def tile_list_stroke_circuit_evidence_kernel(
         offsets = keep.tile([P, S // 16], U16, name="offsets")
         nc.sync.dma_start(offsets[:], offs)
 
-        tab_sc = sb("tab_sc", [P, T], U8, tag="first")
+        tab_sc = sb("tab_sc", [P, T], U8)
         nc.vector.memset(tab_sc[:].bitcast(I32), 0)
         w_sc_raw = sb("w_sc_raw", [P, PASSES, N], U8)
         nc.vector.memset(w_sc_raw[:].bitcast(I32), 0)
         v_sc1 = sb("v_sc1", [P, S], U8)
         nc.vector.memset(v_sc1[:].bitcast(I32), 0)
 
-        wp_raw = sb("wp_raw", [P, PASSES, 2 * N], U8, tag="third")
+        wp_raw = sb("wp_raw", [P, PASSES, 2 * N], U8)
         nc.sync.dma_start(wp_raw[:].bitcast(I32), wp_words.rearrange("a p c -> p a c").bitcast(I32))
-        tab0 = sb("tab0", [P, T], I32, tag="second")
-        nc.sync.dma_start(tab0[:], tab_words[0].rearrange("p c i -> p (c i)").bitcast(I32))
-        g_sb = sb("g_sb", [P, PACK], F32)
-        nc.scalar.dma_start(g_sb[:], g.rearrange("(p t) -> p t", t=PACK))
-        gain_sb = sb("gain_sb", [P, PACK], F32)
-        nc.scalar.dma_start(gain_sb[:], gain.rearrange("(p t) -> p t", t=PACK))
+        tab0 = sb("tab0", [P, T], I32)
+        tab1 = sb("tab1", [P, T], I32)
+        tab0_hbm = tab_words[0].rearrange("p c i -> p (c i)").bitcast(I32)
+        nc.sync.dma_start(tab0[:, 0:LEAD], tab0_hbm[:, 0:LEAD])
         for q in range(4):
-            nc.scalar.dma_start(
+            nc.sync.dma_start(
                 tab_sc[32 * q : 32 * q + 8, :].bitcast(I32), tab_scales[:, 4 * q : 4 * q + 4, :].bitcast(I32)
             )
+        nc.sync.dma_start(tab0[:, LEAD:T], tab0_hbm[:, LEAD:T])
         for q in range(4):
-            nc.scalar.dma_start(
+            nc.sync.dma_start(
                 w_sc_raw[32 * q : 32 * q + 4, :, :].bitcast(I32),
                 wp_scales[:, 4 * q : 4 * q + 4, :].rearrange("a r n -> r a n").bitcast(I32),
             )
+        g_sb = sb("g_sb", [P, PACK], F32)
+        nc.sync.dma_start(g_sb[:], g.rearrange("(p t) -> p t", t=PACK))
+        gain_sb = sb("gain_sb", [P, PACK], F32)
+        nc.sync.dma_start(gain_sb[:], gain.rearrange("(p t) -> p t", t=PACK))
+        nc.sync.dma_start(tab1[:], tab_words[1].rearrange("p c i -> p (c i)").bitcast(I32))
 
         log_g = sb("log_g", [P, PACK], F32)
         nc.scalar.activation(log_g[:], g_sb[:], ACT.Ln)
@@ -80,19 +85,17 @@ def tile_list_stroke_circuit_evidence_kernel(
             out=wp[:].bitcast(U16).rearrange("p a (t c i) -> p a c t i", t=PACK, i=8),
             in_=wp_raw[:].bitcast(U16).rearrange("p a (c i t) -> p a c t i", t=PACK, i=8),
         )
-        tab1 = sb("tab1", [P, T], I32, tag="third")
-        nc.sync.dma_start(tab1[:], tab_words[1].rearrange("p c i -> p (c i)").bitcast(I32))
-
         v_sc = sb("v_sc", [P, S], U8)
         nc.vector.tensor_copy(v_sc[:], tab_sc[:].indirect(offsets[:]))
-        nc.scalar.dma_start(v_sc1[0:112, :].bitcast(I32), v_sc[4:116, :].bitcast(I32))
-        we_raw = [sb("we_raw0", [P, PACK, H], F32, tag="first")]
-        nc.sync.dma_start(we_raw[0][:], we[0:512, :].rearrange("(p j) r -> p j r", j=PACK))
+        nc.sync.dma_start(v_sc1[0:112, :].bitcast(I32), v_sc[4:116, :].bitcast(I32))
+        we_raw = [sb("we_raw%d" % a, [P, PACK, H], F32) for a in range(PASSES)]
+        for a in range(PASSES):
+            nc.sync.dma_start(we_raw[a][:], we[512 * a : 512 * (a + 1), :].rearrange("(p j) r -> p j r", j=PACK))
+        wm_raw = sb("wm_raw", [P, N], I32)
+        nc.sync.dma_start(wm_raw[:], wm_words[0].rearrange("p c i -> p (c i)").bitcast(I32))
 
         v0 = sb("v0", [P, S], U32)
         nc.vector.tensor_copy(v0[:], tab0[:].bitcast(U32).indirect(offsets[:]))
-        we_raw.append(sb("we_raw1", [P, PACK, H], F32, tag="second"))
-        nc.sync.dma_start(we_raw[1][:], we[512:1024, :].rearrange("(p j) r -> p j r", j=PACK))
 
         wp_sc = sb("wp_sc", [P, PASSES, N], U8)
         nc.vector.tensor_copy(
@@ -107,8 +110,6 @@ def tile_list_stroke_circuit_evidence_kernel(
         v1 = [sb("v1_%d" % h, [P, HALF], U32) for h in range(HALVES)]
         for h in range(HALVES):
             nc.vector.tensor_copy(v1[h][:], tab1[:].bitcast(U32).indirect(offsets[:, 32 * h : 32 * (h + 1)]))
-        wm_raw = sb("wm_raw", [P, N], I32, tag="third")
-        nc.sync.dma_start(wm_raw[:], wm_words[0].rearrange("p c i -> p (c i)").bitcast(I32))
 
         def v_words(a, h):
             return (v0[:, HALF * h : HALF * (h + 1)] if a == 0 else v1[h][:]).bitcast(FP8X4)
@@ -186,15 +187,12 @@ def tile_list_stroke_circuit_evidence_kernel(
             )
             leaf_q.append((codes, scales))
 
-        clock = sb("clock", [P, 16], F32)
-        nc.gpsimd.tensor_copy(clock[:, 0:1], prior[1][3][:, 0:1])
-        nc.gpsimd.tensor_copy(clock[:, 8:9], rows[:, 3, 0:1])
         out_rows = out_0.rearrange("(p t) j -> p t j", t=PACK)
         y = []
         for h in range(HALVES):
             y.append(sb("y%d" % h, [P, PACK, HALF], F32))
             for t in range(PACK):
-                mix = bank(7 - t if h == 0 else t)
+                mix = bank(PACK * h + t)
                 nc.tensor.matmul_mx(
                     mix[:],
                     lhsT=wm[:, P * t : P * (t + 1)].bitcast(FP8X4),

@@ -23,6 +23,7 @@ HALF = 512
 HALVES = 2
 QUARTER = 256
 LEAD = 1024
+WE_PIECES = ((0, 0, 512), (1, 0, 256), (1, 256, 512))
 
 
 def interleave(copy, dst, src):
@@ -59,10 +60,9 @@ def tile_list_stroke_circuit_evidence_kernel(
         tab1 = sb("tab1", [P, T], I32)
         tab0_hbm = tab_words[0].rearrange("p c i -> p (c i)").bitcast(I32)
         nc.sync.dma_start(tab0[:, 0:LEAD], tab0_hbm[:, 0:LEAD])
-        for q in range(4):
-            nc.sync.dma_start(
-                tab_sc[32 * q : 32 * q + 8, :].bitcast(I32), tab_scales[:, 4 * q : 4 * q + 4, :].bitcast(I32)
-            )
+        tab_sc_hbm = tab_scales.bitcast(I32).rearrange("a (q r) c -> r q a c", r=4)
+        for r in range(4):
+            nc.sync.dma_start(tab_sc[r:P:16, :].bitcast(I32), tab_sc_hbm[r])
         nc.sync.dma_start(tab0[:, LEAD:T], tab0_hbm[:, LEAD:T])
         for q in range(4):
             nc.sync.dma_start(
@@ -87,10 +87,12 @@ def tile_list_stroke_circuit_evidence_kernel(
         )
         v_sc = sb("v_sc", [P, S], U8)
         nc.vector.tensor_copy(v_sc[:], tab_sc[:].indirect(offsets[:]))
-        nc.sync.dma_start(v_sc1[0:112, :].bitcast(I32), v_sc[4:116, :].bitcast(I32))
-        we_raw = [sb("we_raw%d" % a, [P, PACK, H], F32) for a in range(PASSES)]
-        for a in range(PASSES):
-            nc.sync.dma_start(we_raw[a][:], we[512 * a : 512 * (a + 1), :].rearrange("(p j) r -> p j r", j=PACK))
+        nc.sync.dma_start(v_sc1[0:112, :].bitcast(I32), v_sc[16:P, :].bitcast(I32))
+        we_raw = []
+        for a, lo, hi in WE_PIECES:
+            piece = sb("we_raw%d_%d" % (a, lo), [P, PACK, hi - lo], F32)
+            nc.sync.dma_start(piece[:], we[512 * a : 512 * (a + 1), lo:hi].rearrange("(p j) r -> p j r", j=PACK))
+            we_raw.append(piece)
         wm_raw = sb("wm_raw", [P, N], I32)
         nc.sync.dma_start(wm_raw[:], wm_words[0].rearrange("p c i -> p (c i)").bitcast(I32))
 
@@ -127,25 +129,37 @@ def tile_list_stroke_circuit_evidence_kernel(
                         start=(a == 0),
                         stop=(a == PASSES - 1),
                     )
-        prior = [[sb("prior%d_%d" % (h, t), [P, HALF], F32) for t in range(PACK)] for h in range(HALVES)]
-        for h in range(HALVES):
-            for t in range(PACK):
-                nc.scalar.activation(prior[h][t][:], acc[h][t][:], ACT.Copy, scale=gain_sb[:, t : t + 1])
+        prior = {}
+        for t in range(PACK):
+            prior[0, t] = sb("prior0_%d" % t, [P, HALF], F32)[:]
+            nc.scalar.activation(prior[0, t], acc[0][t][:], ACT.Copy, scale=gain_sb[:, t : t + 1])
 
         we_q = {}
         for a in range(PASSES):
+            grouped = [sb("we_g%d_%d" % (a, u), [P, 2, P, PACK], BF16) for u in range(2)]
+            for piece, (b, lo, hi) in zip(we_raw, WE_PIECES):
+                if b == a:
+                    copy = nc.scalar.copy if (b, lo) == (1, 0) else nc.vector.tensor_copy
+                    for u in range(2):
+                        copy(
+                            out=grouped[u][:, :, lo // PACK : hi // PACK, :].rearrange("p t m j -> p m j t"),
+                            in_=piece[:].rearrange("p j (m t) -> p m j t", t=PACK)[:, :, :, 2 * u : 2 * u + 2],
+                        )
             for u in range(2):
-                grouped = sb("we_g%d_%d" % (a, u), [P, 2, P, PACK], BF16)
-                nc.vector.tensor_copy(
-                    out=grouped[:].rearrange("p t m j -> p m t j"),
-                    in_=we_raw[a][:].rearrange("p j (m t) -> p m t j", t=PACK)[:, :, 2 * u : 2 * u + 2, :],
-                )
                 codes = sb("we_c%d_%d" % (a, u), [P, 2 * P], U32)
                 scales = sb("we_s%d_%d" % (a, u), [P, 2 * P], U8)
                 nc.vector.quantize_mx(
-                    out=codes[:].bitcast(FP8X4), scales=scales[:], in_=grouped[:].rearrange("p t m j -> p (t m j)")
+                    out=codes[:].bitcast(FP8X4), scales=scales[:], in_=grouped[u][:].rearrange("p t m j -> p (t m j)")
                 )
                 we_q[a, u] = (codes, scales)
+
+        prior[1, 0] = sb("prior1_0", [P, HALF], F32)[:]
+        nc.scalar.activation(prior[1, 0], acc[1][0][:], ACT.Copy, scale=gain_sb[:, 0:1])
+        prior[1, 1] = sb("prior1_1", [P, HALF], F32, tag="we_g1_0")[:]
+        late = sb("prior1_2", [P, 2, HALF], F32, tag="we_g1_1")
+        prior[1, 2], prior[1, 3] = late[:, 0, :], late[:, 1, :]
+        for t in range(1, PACK):
+            nc.vector.tensor_scalar(prior[1, t], acc[1][t][:], gain_sb[:, t : t + 1], None, ALU.mult)
 
         wm = sb("wm", [P, N], I32)
         nc.vector.tensor_copy(
@@ -169,16 +183,18 @@ def tile_list_stroke_circuit_evidence_kernel(
                         lhsT=codes[:, cols].bitcast(FP8X4),
                         lhsT_scale=scales[:, cols],
                         rhs=v_words(a, h),
-                        rhs_scale=v_sc[4 * a : P, HALF * h : HALF * (h + 1)],
+                        rhs_scale=(v_sc if a == 0 else v_sc1)[:, HALF * h : HALF * (h + 1)],
                         start=(a == 0),
                         stop=(a == PASSES - 1),
                     )
         leaf_q = []
+        all_rows = []
         for h in range(HALVES):
             rows = sb("leaf_rows%d" % h, [P, PACK, HALF], BF16)
+            all_rows.append(rows)
             for t in range(PACK):
                 nc.scalar.activation(rows[:, t, :], acc[h][t][:], ACT.Exp, bias=log_g[:, t : t + 1])
-            grouped = sb("leaf_g%d" % h, [P, HALF, PACK], BF16)
+            grouped = sb("leaf_g%d" % h, [P, HALF, PACK], BF16, tag="y%d" % (1 - h))
             interleave(nc.vector.tensor_copy, grouped[:], rows[:])
             codes = sb("leaf_c%d" % h, [P, HALF], U32)
             scales = sb("leaf_s%d" % h, [P, HALF], U8)
@@ -205,7 +221,7 @@ def tile_list_stroke_circuit_evidence_kernel(
                 log_mix = sb("log_mix%d_%d" % (h, t), [P, HALF], F32)
                 nc.scalar.activation(log_mix[:], mix[:], ACT.Ln)
                 nc.vector.scalar_tensor_tensor(
-                    y[h][:, t, :], log_mix[:], gain_sb[:, t : t + 1], prior[h][t][:], ALU.mult, ALU.add
+                    y[h][:, t, :], log_mix[:], gain_sb[:, t : t + 1], prior[h, t], ALU.mult, ALU.add
                 )
                 if t % 2 == 1:
                     nc.sync.dma_start(

@@ -23,7 +23,6 @@ HALF = 512
 HALVES = 2
 QUARTER = 256
 LEAD = 1024
-WE_PIECES = ((0, 0, 512), (1, 0, 256), (1, 256, 512))
 
 
 def interleave(copy, dst, src):
@@ -88,11 +87,9 @@ def tile_list_stroke_circuit_evidence_kernel(
         v_sc = sb("v_sc", [P, S], U8)
         nc.vector.tensor_copy(v_sc[:], tab_sc[:].indirect(offsets[:]))
         nc.sync.dma_start(v_sc1[0:112, :].bitcast(I32), v_sc[16:P, :].bitcast(I32))
-        we_raw = []
-        for a, lo, hi in WE_PIECES:
-            piece = sb("we_raw%d_%d" % (a, lo), [P, PACK, hi - lo], F32)
-            nc.sync.dma_start(piece[:], we[512 * a : 512 * (a + 1), lo:hi].rearrange("(p j) r -> p j r", j=PACK))
-            we_raw.append(piece)
+        we_raw = [sb("we_raw%d" % a, [P, PACK, H], F32) for a in range(PASSES)]
+        for a in range(PASSES):
+            nc.sync.dma_start(we_raw[a][:], we[512 * a : 512 * (a + 1), :].rearrange("(p j) r -> p j r", j=PACK))
         wm_raw = sb("wm_raw", [P, N], I32)
         nc.sync.dma_start(wm_raw[:], wm_words[0].rearrange("p c i -> p (c i)").bitcast(I32))
 
@@ -136,20 +133,16 @@ def tile_list_stroke_circuit_evidence_kernel(
 
         we_q = {}
         for a in range(PASSES):
-            grouped = [sb("we_g%d_%d" % (a, u), [P, 2, P, PACK], BF16) for u in range(2)]
-            for piece, (b, lo, hi) in zip(we_raw, WE_PIECES):
-                if b == a:
-                    copy = nc.scalar.copy if (b, lo) == (1, 0) else nc.vector.tensor_copy
-                    for u in range(2):
-                        copy(
-                            out=grouped[u][:, :, lo // PACK : hi // PACK, :].rearrange("p t m j -> p m j t"),
-                            in_=piece[:].rearrange("p j (m t) -> p m j t", t=PACK)[:, :, :, 2 * u : 2 * u + 2],
-                        )
             for u in range(2):
+                grouped = sb("we_g%d_%d" % (a, u), [P, 2, P, PACK], BF16)
+                (nc.scalar.copy if (a, u) == (1, 1) else nc.vector.tensor_copy)(
+                    out=grouped[:].rearrange("p t m j -> p m j t"),
+                    in_=we_raw[a][:].rearrange("p j (m t) -> p m j t", t=PACK)[:, :, :, 2 * u : 2 * u + 2],
+                )
                 codes = sb("we_c%d_%d" % (a, u), [P, 2 * P], U32)
                 scales = sb("we_s%d_%d" % (a, u), [P, 2 * P], U8)
                 nc.vector.quantize_mx(
-                    out=codes[:].bitcast(FP8X4), scales=scales[:], in_=grouped[u][:].rearrange("p t m j -> p (t m j)")
+                    out=codes[:].bitcast(FP8X4), scales=scales[:], in_=grouped[:].rearrange("p t m j -> p (t m j)")
                 )
                 we_q[a, u] = (codes, scales)
 

@@ -22,7 +22,9 @@ PASSES = 2
 HALF = 512
 HALVES = 2
 QUARTER = 256
-LEAD = 1024
+LEAD = 768
+LAST = 3328
+CUT = 1792
 
 
 def interleave(copy, dst, src):
@@ -50,29 +52,33 @@ def tile_list_stroke_circuit_evidence_kernel(
         nc.vector.memset(tab_sc[:].bitcast(I32), 0)
         w_sc_raw = sb("w_sc_raw", [P, PASSES, N], U8)
         nc.vector.memset(w_sc_raw[:].bitcast(I32), 0)
-        v_sc1 = sb("v_sc1", [P, S], U8)
-        nc.vector.memset(v_sc1[:].bitcast(I32), 0)
+        wm_sc = sb("wm_sc", [P, N], U8)
+        nc.vector.memset(wm_sc[:].bitcast(I32), 0)
+        v_sc = [sb("v_sc%d" % a, [P, S], U8) for a in range(PASSES)]
+        for a in range(PASSES):
+            nc.vector.memset(v_sc[a][:].bitcast(I32), 0)
 
+        g_sb = sb("g_sb", [P, PACK], F32)
+        nc.scalar.dma_start(g_sb[:], g.rearrange("(p t) -> p t", t=PACK))
+        gain_sb = sb("gain_sb", [P, PACK], F32)
+        nc.scalar.dma_start(gain_sb[:], gain.rearrange("(p t) -> p t", t=PACK))
         wp_raw = sb("wp_raw", [P, PASSES, 2 * N], U8)
         nc.sync.dma_start(wp_raw[:].bitcast(I32), wp_words.rearrange("a p c -> p a c").bitcast(I32))
         tab0 = sb("tab0", [P, T], I32)
         tab1 = sb("tab1", [P, T], I32)
         tab0_hbm = tab_words[0].rearrange("p c i -> p (c i)").bitcast(I32)
         nc.sync.dma_start(tab0[:, 0:LEAD], tab0_hbm[:, 0:LEAD])
-        tab_sc_hbm = tab_scales.bitcast(I32).rearrange("a (q r) c -> r q a c", r=4)
-        for r in range(4):
-            nc.sync.dma_start(tab_sc[r:P:16, :].bitcast(I32), tab_sc_hbm[r])
-        nc.sync.dma_start(tab0[:, LEAD:T], tab0_hbm[:, LEAD:T])
+        nc.sync.dma_start(tab_sc[0:P:4, :].bitcast(I32), tab_scales.bitcast(I32).rearrange("a i c -> (a i) c"))
+        nc.sync.dma_start(tab0[:, LEAD:LAST], tab0_hbm[:, LEAD:LAST])
         for q in range(4):
             nc.sync.dma_start(
                 w_sc_raw[32 * q : 32 * q + 4, :, :].bitcast(I32),
                 wp_scales[:, 4 * q : 4 * q + 4, :].rearrange("a r n -> r a n").bitcast(I32),
             )
-        g_sb = sb("g_sb", [P, PACK], F32)
-        nc.sync.dma_start(g_sb[:], g.rearrange("(p t) -> p t", t=PACK))
-        gain_sb = sb("gain_sb", [P, PACK], F32)
-        nc.sync.dma_start(gain_sb[:], gain.rearrange("(p t) -> p t", t=PACK))
-        nc.sync.dma_start(tab1[:], tab_words[1].rearrange("p c i -> p (c i)").bitcast(I32))
+        nc.sync.dma_start(w_sc_raw[4:P:8, 0, :].bitcast(I32), wm_scales[0].bitcast(I32))
+        nc.sync.dma_start(tab0[:, LAST:T], tab0_hbm[:, LAST:T])
+        tab1_hbm = tab_words[1].rearrange("p c i -> p (c i)").bitcast(I32)
+        nc.sync.dma_start(tab1[:, 0:CUT], tab1_hbm[:, 0:CUT])
 
         log_g = sb("log_g", [P, PACK], F32)
         nc.scalar.activation(log_g[:], g_sb[:], ACT.Ln)
@@ -84,34 +90,39 @@ def tile_list_stroke_circuit_evidence_kernel(
             out=wp[:].bitcast(U16).rearrange("p a (t c i) -> p a c t i", t=PACK, i=8),
             in_=wp_raw[:].bitcast(U16).rearrange("p a (c i t) -> p a c t i", t=PACK, i=8),
         )
-        v_sc = sb("v_sc", [P, S], U8)
-        nc.vector.tensor_copy(v_sc[:], tab_sc[:].indirect(offsets[:]))
-        nc.sync.dma_start(v_sc1[0:112, :].bitcast(I32), v_sc[16:P, :].bitcast(I32))
+        picked_sc = sb("picked_sc", [P, S], U8)
+        nc.vector.tensor_copy(picked_sc[:], tab_sc[:].indirect(offsets[:]))
+        for a in range(PASSES):
+            for r in range(4):
+                nc.sync.dma_start(
+                    v_sc[a][r:P:32, :].bitcast(I32),
+                    picked_sc[64 * a + 4 * r : 64 * (a + 1) : 16, :].bitcast(I32),
+                )
+            if a == 0:
+                nc.sync.dma_start(tab1[:, CUT:T], tab1_hbm[:, CUT:T])
         we_raw = [sb("we_raw%d" % a, [P, PACK, H], F32) for a in range(PASSES)]
         for a in range(PASSES):
             nc.sync.dma_start(we_raw[a][:], we[512 * a : 512 * (a + 1), :].rearrange("(p j) r -> p j r", j=PACK))
         wm_raw = sb("wm_raw", [P, N], I32)
         nc.sync.dma_start(wm_raw[:], wm_words[0].rearrange("p c i -> p (c i)").bitcast(I32))
 
-        v0 = sb("v0", [P, S], U32)
-        nc.vector.tensor_copy(v0[:], tab0[:].bitcast(U32).indirect(offsets[:]))
-
         wp_sc = sb("wp_sc", [P, PASSES, N], U8)
         nc.vector.tensor_copy(
             out=wp_sc[:].rearrange("p a (t c i) -> p a c t i", t=PACK, i=16),
             in_=w_sc_raw[:].rearrange("p a (c i t) -> p a c t i", t=PACK, i=16),
         )
-        wm_sc_raw = w_sc_raw[:, 0, :]
-        for q in range(4):
-            nc.sync.dma_start(
-                w_sc_raw[32 * q : 32 * q + 4, 0, :].bitcast(I32), wm_scales[0, 4 * q : 4 * q + 4, :].bitcast(I32)
-            )
+        for r in range(4):
+            nc.sync.dma_start(wm_sc[r:P:32, :].bitcast(I32), wp_sc[8 * r + 4 : P : 32, 0, :].bitcast(I32))
+        v0 = [sb("v0_%d" % h, [P, HALF], U32) for h in range(HALVES)]
+        for h in range(HALVES):
+            nc.vector.tensor_copy(v0[h][:], tab0[:].bitcast(U32).indirect(offsets[:, 32 * h : 32 * (h + 1)]))
+
         v1 = [sb("v1_%d" % h, [P, HALF], U32) for h in range(HALVES)]
         for h in range(HALVES):
             nc.vector.tensor_copy(v1[h][:], tab1[:].bitcast(U32).indirect(offsets[:, 32 * h : 32 * (h + 1)]))
 
         def v_words(a, h):
-            return (v0[:, HALF * h : HALF * (h + 1)] if a == 0 else v1[h][:]).bitcast(FP8X4)
+            return (v0 if a == 0 else v1)[h][:].bitcast(FP8X4)
 
         acc = [[bank(PACK * h + t) for t in range(PACK)] for h in range(HALVES)]
         for a in range(PASSES):
@@ -122,7 +133,7 @@ def tile_list_stroke_circuit_evidence_kernel(
                         lhsT=wp[:, a, 2 * P * t : 2 * P * (t + 1)].bitcast(FP4X4),
                         lhsT_scale=wp_sc[:, a, P * t : P * (t + 1)],
                         rhs=v_words(a, h),
-                        rhs_scale=(v_sc if a == 0 else v_sc1)[:, HALF * h : HALF * (h + 1)],
+                        rhs_scale=v_sc[a][:, HALF * h : HALF * (h + 1)],
                         start=(a == 0),
                         stop=(a == PASSES - 1),
                     )
@@ -133,12 +144,14 @@ def tile_list_stroke_circuit_evidence_kernel(
 
         we_q = {}
         for a in range(PASSES):
+            pairs = [sb("we_g%d_%d" % (a, u), [P, 2, P, PACK], BF16) for u in range(2)]
             for u in range(2):
-                grouped = sb("we_g%d_%d" % (a, u), [P, 2, P, PACK], BF16)
                 (nc.scalar.copy if (a, u) == (1, 1) else nc.vector.tensor_copy)(
-                    out=grouped[:].rearrange("p t m j -> p m j t"),
+                    out=pairs[u][:].rearrange("p t m j -> p m j t"),
                     in_=we_raw[a][:].rearrange("p j (m t) -> p m j t", t=PACK)[:, :, :, 2 * u : 2 * u + 2],
                 )
+            for u in range(2):
+                grouped = pairs[u]
                 codes = sb("we_c%d_%d" % (a, u), [P, 2 * P], U32)
                 scales = sb("we_s%d_%d" % (a, u), [P, 2 * P], U8)
                 nc.vector.quantize_mx(
@@ -159,16 +172,14 @@ def tile_list_stroke_circuit_evidence_kernel(
             out=wm[:].rearrange("p (t c i) -> p c t i", t=PACK, i=4),
             in_=wm_raw[:].rearrange("p (c i t) -> p c t i", t=PACK, i=4),
         )
-        wm_sc = sb("wm_sc", [P, N], U8)
-        nc.vector.tensor_copy(
-            out=wm_sc[:].rearrange("p (t c i) -> p c t i", t=PACK, i=16),
-            in_=wm_sc_raw.rearrange("p (c i t) -> p c t i", t=PACK, i=16),
-        )
 
         acc = [[bank(PACK * h + t) for t in range(PACK)] for h in range(HALVES)]
         for h in range(HALVES):
-            for a in range(PASSES):
-                for t in range(PACK):
+            order = [(a, t) for a in range(PASSES) for t in range(PACK)]
+            if h == 1:
+                order = [(a, t) for t in range(PACK) for a in range(PASSES)]
+            for a, t in order:
+                if True:
                     codes, scales = we_q[a, t // 2]
                     cols = slice(P * (t % 2), P * (t % 2 + 1))
                     nc.tensor.matmul_mx(
@@ -176,7 +187,7 @@ def tile_list_stroke_circuit_evidence_kernel(
                         lhsT=codes[:, cols].bitcast(FP8X4),
                         lhsT_scale=scales[:, cols],
                         rhs=v_words(a, h),
-                        rhs_scale=(v_sc if a == 0 else v_sc1)[:, HALF * h : HALF * (h + 1)],
+                        rhs_scale=v_sc[a][:, HALF * h : HALF * (h + 1)],
                         start=(a == 0),
                         stop=(a == PASSES - 1),
                     )
@@ -188,12 +199,17 @@ def tile_list_stroke_circuit_evidence_kernel(
             for t in range(PACK):
                 nc.scalar.activation(rows[:, t, :], acc[h][t][:], ACT.Exp, bias=log_g[:, t : t + 1])
             grouped = sb("leaf_g%d" % h, [P, HALF, PACK], BF16, tag="y%d" % (1 - h))
-            interleave(nc.vector.tensor_copy, grouped[:], rows[:])
             codes = sb("leaf_c%d" % h, [P, HALF], U32)
             scales = sb("leaf_s%d" % h, [P, HALF], U8)
-            nc.vector.quantize_mx(
-                out=codes[:].bitcast(FP8X4), scales=scales[:], in_=grouped[:].rearrange("p j t -> p (j t)")
-            )
+            quarters = [slice(0, QUARTER), slice(QUARTER, HALF)]
+            for cols in quarters:
+                interleave(nc.vector.tensor_copy, grouped[:, cols, :], rows[:, :, cols])
+            for cols in quarters:
+                nc.vector.quantize_mx(
+                    out=codes[:, cols].bitcast(FP8X4),
+                    scales=scales[:, cols],
+                    in_=grouped[:, cols, :].rearrange("p j t -> p (j t)"),
+                )
             leaf_q.append((codes, scales))
 
         out_rows = out_0.rearrange("(p t) j -> p t j", t=PACK)
@@ -223,17 +239,17 @@ def tile_list_stroke_circuit_evidence_kernel(
 
         out_words = out_1[0].rearrange("p m t -> p (m t)").bitcast(I32)
         y_sc = sb("y_sc", [P, S], U8)
-        for name, copy, h, lo, width in (
-            ("a", nc.scalar.copy, 0, 0, QUARTER),
-            ("b", nc.vector.tensor_copy, 1, 0, HALF),
-            ("c", nc.scalar.copy, 0, QUARTER, QUARTER),
-        ):
-            grouped = sb("y_g" + name, [P, width, PACK], BF16)
-            interleave(copy, grouped[:], y[h][:, :, lo : lo + width])
+        y_g = [sb("y_g%d" % h, [P, HALF, PACK], BF16) for h in range(HALVES)]
+        for h in range(HALVES):
+            interleave(nc.scalar.copy, y_g[h][:, 0:QUARTER, :], y[h][:, :, 0:QUARTER])
+            interleave(nc.vector.tensor_copy, y_g[h][:, QUARTER:HALF, :], y[h][:, :, QUARTER:HALF])
+        for name, h, lo, width in (("a", 0, 0, HALF), ("b", 1, QUARTER, QUARTER), ("c", 1, 0, QUARTER)):
             codes = sb("y_c" + name, [P, width], I32)
             cols = slice(HALF * h + lo, HALF * h + lo + width)
             nc.vector.quantize_mx(
-                out=codes[:].bitcast(FP8X4), scales=y_sc[:, cols], in_=grouped[:].rearrange("p j t -> p (j t)")
+                out=codes[:].bitcast(FP8X4),
+                scales=y_sc[:, cols],
+                in_=y_g[h][:, lo : lo + width, :].rearrange("p j t -> p (j t)"),
             )
             nc.sync.dma_start(out_words[:, cols], codes[:])
         for q in range(4):

@@ -22,9 +22,12 @@ PASSES = 2
 HALF = 512
 HALVES = 2
 QUARTER = 256
-LEAD = 768
-LAST = 3328
-CUT = 1792
+SHARE = 320
+SPLIT = 64
+FIRST = 88
+LEAD = 2048
+CUT = 2816
+ROWS = 96
 
 
 def interleave(copy, dst, src):
@@ -46,10 +49,11 @@ def tile_list_stroke_circuit_evidence_kernel(
             return psum.tile([P, HALF], F32, name="bank%d" % b)
 
         offsets = keep.tile([P, S // 16], U16, name="offsets")
-        nc.sync.dma_start(offsets[:], offs)
 
         tab_sc = sb("tab_sc", [P, T], U8)
-        nc.vector.memset(tab_sc[:].bitcast(I32), 0)
+        nc.vector.memset(tab_sc[0:ROWS, :].bitcast(I32), 0)
+        nc.sync.dma_start(tab_sc[ROWS:P, :].bitcast(I32), tab_scales.bitcast(I32).rearrange("a i c -> (a i) c"))
+        nc.sync.dma_start(offsets[:], offs)
         w_sc_raw = sb("w_sc_raw", [P, PASSES, N], U8)
         nc.vector.memset(w_sc_raw[:].bitcast(I32), 0)
         wm_sc = sb("wm_sc", [P, N], U8)
@@ -60,25 +64,27 @@ def tile_list_stroke_circuit_evidence_kernel(
 
         g_sb = sb("g_sb", [P, PACK], F32)
         nc.scalar.dma_start(g_sb[:], g.rearrange("(p t) -> p t", t=PACK))
-        gain_sb = sb("gain_sb", [P, PACK], F32)
-        nc.scalar.dma_start(gain_sb[:], gain.rearrange("(p t) -> p t", t=PACK))
+        gains = [sb("gain0", [P, 3], F32), sb("gain1", [P, 1], F32)]
+        gain_hbm = gain.rearrange("(p t) -> p t", t=PACK)
+        nc.scalar.dma_start(gains[0][:], gain_hbm[:, 0:3])
+
+        def gain_of(t):
+            return gains[t // 3][:, t % 3 : t % 3 + 1]
+
         wp_raw = sb("wp_raw", [P, PASSES, 2 * N], U8)
-        nc.sync.dma_start(wp_raw[:].bitcast(I32), wp_words.rearrange("a p c -> p a c").bitcast(I32))
         tab0 = sb("tab0", [P, T], I32)
         tab1 = sb("tab1", [P, T], I32)
         tab0_hbm = tab_words[0].rearrange("p c i -> p (c i)").bitcast(I32)
         nc.sync.dma_start(tab0[:, 0:LEAD], tab0_hbm[:, 0:LEAD])
-        nc.sync.dma_start(tab_sc[0:P:4, :].bitcast(I32), tab_scales.bitcast(I32).rearrange("a i c -> (a i) c"))
-        nc.sync.dma_start(tab0[:, LEAD:LAST], tab0_hbm[:, LEAD:LAST])
+        nc.sync.dma_start(wp_raw[:].bitcast(I32), wp_words.rearrange("a p c -> p a c").bitcast(I32))
         for q in range(4):
             nc.sync.dma_start(
                 w_sc_raw[32 * q : 32 * q + 4, :, :].bitcast(I32),
                 wp_scales[:, 4 * q : 4 * q + 4, :].rearrange("a r n -> r a n").bitcast(I32),
             )
         nc.sync.dma_start(w_sc_raw[4:P:8, 0, :].bitcast(I32), wm_scales[0].bitcast(I32))
-        nc.sync.dma_start(tab0[:, LAST:T], tab0_hbm[:, LAST:T])
+        nc.sync.dma_start(tab0[:, LEAD:T], tab0_hbm[:, LEAD:T])
         tab1_hbm = tab_words[1].rearrange("p c i -> p (c i)").bitcast(I32)
-        nc.sync.dma_start(tab1[:, 0:CUT], tab1_hbm[:, 0:CUT])
 
         log_g = sb("log_g", [P, PACK], F32)
         nc.scalar.activation(log_g[:], g_sb[:], ACT.Ln)
@@ -96,13 +102,15 @@ def tile_list_stroke_circuit_evidence_kernel(
             for r in range(4):
                 nc.sync.dma_start(
                     v_sc[a][r:P:32, :].bitcast(I32),
-                    picked_sc[64 * a + 4 * r : 64 * (a + 1) : 16, :].bitcast(I32),
+                    picked_sc[ROWS + 16 * a + r : ROWS + 16 * (a + 1) : 4, :].bitcast(I32),
                 )
-            if a == 0:
-                nc.sync.dma_start(tab1[:, CUT:T], tab1_hbm[:, CUT:T])
+            lo, hi = ((0, CUT), (CUT, T))[a]
+            nc.sync.dma_start(tab1[:, lo:hi], tab1_hbm[:, lo:hi])
         we_raw = [sb("we_raw%d" % a, [P, PACK, H], F32) for a in range(PASSES)]
         for a in range(PASSES):
             nc.sync.dma_start(we_raw[a][:], we[512 * a : 512 * (a + 1), :].rearrange("(p j) r -> p j r", j=PACK))
+        with nc.allow_non_contiguous_dma(reason="one value a partition"):
+            nc.sync.dma_start(gains[1][:], gain_hbm[:, 3:4])
         wm_raw = sb("wm_raw", [P, N], I32)
         nc.sync.dma_start(wm_raw[:], wm_words[0].rearrange("p c i -> p (c i)").bitcast(I32))
 
@@ -138,46 +146,53 @@ def tile_list_stroke_circuit_evidence_kernel(
                         stop=(a == PASSES - 1),
                     )
         prior = {}
-        for t in range(PACK):
-            prior[0, t] = sb("prior0_%d" % t, [P, HALF], F32)[:]
-            nc.scalar.activation(prior[0, t], acc[0][t][:], ACT.Copy, scale=gain_sb[:, t : t + 1])
+        for h, t in ((0, 0), (0, 1), (0, 2), (1, 0)):
+            prior[h, t] = sb("prior%d_%d" % (h, t), [P, HALF], F32)[:]
+            nc.scalar.activation(prior[h, t], acc[h][t][:], ACT.Copy, scale=gain_of(t))
 
         we_q = {}
         for a in range(PASSES):
             pairs = [sb("we_g%d_%d" % (a, u), [P, 2, P, PACK], BF16) for u in range(2)]
             for u in range(2):
-                (nc.scalar.copy if (a, u) == (1, 1) else nc.vector.tensor_copy)(
-                    out=pairs[u][:].rearrange("p t m j -> p m j t"),
-                    in_=we_raw[a][:].rearrange("p j (m t) -> p m j t", t=PACK)[:, :, :, 2 * u : 2 * u + 2],
-                )
-            for u in range(2):
-                grouped = pairs[u]
-                codes = sb("we_c%d_%d" % (a, u), [P, 2 * P], U32)
-                scales = sb("we_s%d_%d" % (a, u), [P, 2 * P], U8)
-                nc.vector.quantize_mx(
-                    out=codes[:].bitcast(FP8X4), scales=scales[:], in_=grouped[:].rearrange("p t m j -> p (t m j)")
-                )
-                we_q[a, u] = (codes, scales)
+                we_q[a, u] = (sb("we_c%d_%d" % (a, u), [P, 2 * P], U32), sb("we_s%d_%d" % (a, u), [P, 2 * P], U8))
+            steps = [("v", 0, 0, P), ("v", 1, 0, P), ("q", 0, 0, 2 * P), ("q", 1, 0, 2 * P)]
+            if a == 1:
+                steps = [("v", 0, 0, FIRST), ("s", 0, FIRST, P), ("v", 1, 0, SPLIT), ("q", 0, 0, P), ("q", 0, P, 2 * P)]
+                steps = steps + [("v", 1, SPLIT, P), ("q", 1, 0, 2 * P)]
+            for kind, u, lo, hi in steps:
+                if kind == "q":
+                    codes, scales = we_q[a, u]
+                    nc.vector.quantize_mx(
+                        out=codes[:, lo:hi].bitcast(FP8X4),
+                        scales=scales[:, lo:hi],
+                        in_=pairs[u][:].rearrange("p t m j -> p (t m j)")[:, PACK * lo : PACK * hi],
+                    )
+                else:
+                    (nc.scalar.copy if kind == "s" else nc.vector.tensor_copy)(
+                        out=pairs[u][:].rearrange("p t m j -> p m j t")[:, lo:hi],
+                        in_=we_raw[a][:].rearrange("p j (m t) -> p m j t", t=PACK)[:, lo:hi, :, 2 * u : 2 * u + 2],
+                    )
 
-        prior[1, 0] = sb("prior1_0", [P, HALF], F32)[:]
-        nc.scalar.activation(prior[1, 0], acc[1][0][:], ACT.Copy, scale=gain_sb[:, 0:1])
-        prior[1, 1] = sb("prior1_1", [P, HALF], F32, tag="we_g1_0")[:]
-        late = sb("prior1_2", [P, 2, HALF], F32, tag="we_g1_1")
-        prior[1, 2], prior[1, 3] = late[:, 0, :], late[:, 1, :]
-        for t in range(1, PACK):
-            nc.vector.tensor_scalar(prior[1, t], acc[1][t][:], gain_sb[:, t : t + 1], None, ALU.mult)
+        for h in range(HALVES):
+            prior[h, 3] = sb("prior%d_3" % h, [P, HALF], F32)[:]
+            nc.scalar.activation(prior[h, 3], acc[h][3][:], ACT.Copy, scale=gain_of(3))
+        late = sb("prior1", [P, 2, HALF], F32, tag="we_raw1")
+        for t in range(1, PACK - 1):
+            prior[1, t] = late[:, t - 1, :]
+            nc.vector.tensor_scalar(prior[1, t], acc[1][t][:], gain_of(t), None, ALU.mult)
 
-        wm = sb("wm", [P, N], I32)
-        nc.vector.tensor_copy(
+        wm = sb("wm", [P, N], I32, tag="we_g1_1")
+        nc.gpsimd.tensor_copy(
             out=wm[:].rearrange("p (t c i) -> p c t i", t=PACK, i=4),
             in_=wm_raw[:].rearrange("p (c i t) -> p c t i", t=PACK, i=4),
         )
 
-        acc = [[bank(PACK * h + t) for t in range(PACK)] for h in range(HALVES)]
+        banks = ((0, 1, 2, 4), (5, 6, 3, 7))
+        acc = [[bank(banks[h][t]) for t in range(PACK)] for h in range(HALVES)]
         for h in range(HALVES):
             order = [(a, t) for a in range(PASSES) for t in range(PACK)]
             if h == 1:
-                order = [(a, t) for t in range(PACK) for a in range(PASSES)]
+                order = [(a, t) for t in (2, 3, 0, 1) for a in (1, 0)]
             for a, t in order:
                 if True:
                     codes, scales = we_q[a, t // 2]
@@ -188,15 +203,15 @@ def tile_list_stroke_circuit_evidence_kernel(
                         lhsT_scale=scales[:, cols],
                         rhs=v_words(a, h),
                         rhs_scale=v_sc[a][:, HALF * h : HALF * (h + 1)],
-                        start=(a == 0),
-                        stop=(a == PASSES - 1),
+                        start=(a == h),
+                        stop=(a != h),
                     )
         leaf_q = []
         all_rows = []
         for h in range(HALVES):
             rows = sb("leaf_rows%d" % h, [P, PACK, HALF], BF16)
             all_rows.append(rows)
-            for t in range(PACK):
+            for t in ((0, 1, 2, 3), (2, 3, 0, 1))[h]:
                 nc.scalar.activation(rows[:, t, :], acc[h][t][:], ACT.Exp, bias=log_g[:, t : t + 1])
             grouped = sb("leaf_g%d" % h, [P, HALF, PACK], BF16, tag="y%d" % (1 - h))
             codes = sb("leaf_c%d" % h, [P, HALF], U32)
@@ -217,7 +232,7 @@ def tile_list_stroke_circuit_evidence_kernel(
         for h in range(HALVES):
             y.append(sb("y%d" % h, [P, PACK, HALF], F32))
             for t in range(PACK):
-                mix = bank(PACK * h + t)
+                mix = bank(banks[h][t])
                 nc.tensor.matmul_mx(
                     mix[:],
                     lhsT=wm[:, P * t : P * (t + 1)].bitcast(FP8X4),
@@ -230,7 +245,7 @@ def tile_list_stroke_circuit_evidence_kernel(
                 log_mix = sb("log_mix%d_%d" % (h, t), [P, HALF], F32)
                 nc.scalar.activation(log_mix[:], mix[:], ACT.Ln)
                 nc.vector.scalar_tensor_tensor(
-                    y[h][:, t, :], log_mix[:], gain_sb[:, t : t + 1], prior[h, t], ALU.mult, ALU.add
+                    y[h][:, t, :], log_mix[:], gain_of(t), prior[h, t], ALU.mult, ALU.add
                 )
                 if t % 2 == 1:
                     nc.sync.dma_start(
@@ -240,9 +255,9 @@ def tile_list_stroke_circuit_evidence_kernel(
         out_words = out_1[0].rearrange("p m t -> p (m t)").bitcast(I32)
         y_sc = sb("y_sc", [P, S], U8)
         y_g = [sb("y_g%d" % h, [P, HALF, PACK], BF16) for h in range(HALVES)]
-        for h in range(HALVES):
-            interleave(nc.scalar.copy, y_g[h][:, 0:QUARTER, :], y[h][:, :, 0:QUARTER])
-            interleave(nc.vector.tensor_copy, y_g[h][:, QUARTER:HALF, :], y[h][:, :, QUARTER:HALF])
+        for h, cut in enumerate((SHARE, QUARTER)):
+            interleave(nc.scalar.copy, y_g[h][:, 0:cut, :], y[h][:, :, 0:cut])
+            interleave(nc.vector.tensor_copy, y_g[h][:, cut:HALF, :], y[h][:, :, cut:HALF])
         for name, h, lo, width in (("a", 0, 0, HALF), ("b", 1, QUARTER, QUARTER), ("c", 1, 0, QUARTER)):
             codes = sb("y_c" + name, [P, width], I32)
             cols = slice(HALF * h + lo, HALF * h + lo + width)

@@ -26,7 +26,7 @@ SHARE = 320
 SPLIT = 64
 FIRST = 88
 LEAD = 2048
-CUT = 2816
+CUT = 1536
 ROWS = 96
 
 
@@ -52,15 +52,14 @@ def tile_list_stroke_circuit_evidence_kernel(
 
         tab_sc = sb("tab_sc", [P, T], U8)
         nc.vector.memset(tab_sc[0:ROWS, :].bitcast(I32), 0)
-        nc.sync.dma_start(tab_sc[ROWS:P, :].bitcast(I32), tab_scales.bitcast(I32).rearrange("a i c -> (a i) c"))
+        nc.sync.dma_start(tab_sc[ROWS:P, :].bitcast(I32), tab_scales.bitcast(I32).rearrange("a i c -> i a c"))
         nc.sync.dma_start(offsets[:], offs)
         w_sc_raw = sb("w_sc_raw", [P, PASSES, N], U8)
         nc.vector.memset(w_sc_raw[:].bitcast(I32), 0)
         wm_sc = sb("wm_sc", [P, N], U8)
         nc.vector.memset(wm_sc[:].bitcast(I32), 0)
-        v_sc = [sb("v_sc%d" % a, [P, S], U8) for a in range(PASSES)]
-        for a in range(PASSES):
-            nc.vector.memset(v_sc[a][:].bitcast(I32), 0)
+        v_sc = sb("v_sc", [P, PASSES, S], U8)
+        nc.vector.memset(v_sc[:].bitcast(I32), 0)
 
         g_sb = sb("g_sb", [P, PACK], F32)
         nc.scalar.dma_start(g_sb[:], g.rearrange("(p t) -> p t", t=PACK))
@@ -98,14 +97,13 @@ def tile_list_stroke_circuit_evidence_kernel(
         )
         picked_sc = sb("picked_sc", [P, S], U8)
         nc.vector.tensor_copy(picked_sc[:], tab_sc[:].indirect(offsets[:]))
-        for a in range(PASSES):
-            for r in range(4):
-                nc.sync.dma_start(
-                    v_sc[a][r:P:32, :].bitcast(I32),
-                    picked_sc[ROWS + 16 * a + r : ROWS + 16 * (a + 1) : 4, :].bitcast(I32),
-                )
-            lo, hi = ((0, CUT), (CUT, T))[a]
-            nc.sync.dma_start(tab1[:, lo:hi], tab1_hbm[:, lo:hi])
+        nc.sync.dma_start(tab1[:, 0:CUT], tab1_hbm[:, 0:CUT])
+        for q in range(4):
+            nc.sync.dma_start(
+                v_sc[32 * q : 32 * q + 4, :, :].bitcast(I32),
+                picked_sc[ROWS + 8 * q : ROWS + 8 * (q + 1), :].bitcast(I32),
+            )
+        nc.sync.dma_start(tab1[:, CUT:T], tab1_hbm[:, CUT:T])
         we_raw = [sb("we_raw%d" % a, [P, PACK, H], F32) for a in range(PASSES)]
         for a in range(PASSES):
             nc.sync.dma_start(we_raw[a][:], we[512 * a : 512 * (a + 1), :].rearrange("(p j) r -> p j r", j=PACK))
@@ -141,7 +139,7 @@ def tile_list_stroke_circuit_evidence_kernel(
                         lhsT=wp[:, a, 2 * P * t : 2 * P * (t + 1)].bitcast(FP4X4),
                         lhsT_scale=wp_sc[:, a, P * t : P * (t + 1)],
                         rhs=v_words(a, h),
-                        rhs_scale=v_sc[a][:, HALF * h : HALF * (h + 1)],
+                        rhs_scale=v_sc[:, a, HALF * h : HALF * (h + 1)],
                         start=(a == 0),
                         stop=(a == PASSES - 1),
                     )
@@ -202,7 +200,7 @@ def tile_list_stroke_circuit_evidence_kernel(
                         lhsT=codes[:, cols].bitcast(FP8X4),
                         lhsT_scale=scales[:, cols],
                         rhs=v_words(a, h),
-                        rhs_scale=v_sc[a][:, HALF * h : HALF * (h + 1)],
+                        rhs_scale=v_sc[:, a, HALF * h : HALF * (h + 1)],
                         start=(a == h),
                         stop=(a != h),
                     )

@@ -1,6 +1,7 @@
 from contextlib import ExitStack
 
 import concourse.mybir as mybir
+from concourse.masks import make_identity
 
 K, T, S, H, N = 1024, 4096, 1024, 512, 512
 FLOPS = 2 * S * (K * H + H * N + K * N)
@@ -63,12 +64,19 @@ def tile_list_stroke_circuit_evidence_kernel(
 
         g_sb = sb("g_sb", [P, PACK], F32)
         nc.scalar.dma_start(g_sb[:], g.rearrange("(p t) -> p t", t=PACK))
-        gains = [sb("gain0", [P, 3], F32), sb("gain1", [P, 1], F32)]
-        gain_hbm = gain.rearrange("(p t) -> p t", t=PACK)
-        nc.scalar.dma_start(gains[0][:], gain_hbm[:, 0:3])
+        gain_sb = sb("gain_sb", [P, PACK], F32)
+        nc.scalar.dma_start(gain_sb[:], gain.rearrange("(p t) -> p t", t=PACK))
 
         def gain_of(t):
-            return gains[t // 3][:, t % 3 : t % 3 + 1]
+            return gain_sb[:, t : t + 1]
+
+        ident = sb("ident", [P, P], F32)
+        make_identity(nc, ident[:])
+        spread = bank(7)
+        for t in range(PACK):
+            nc.tensor.transpose(spread[:, P * t : P * (t + 1)], gain_of(t).to_broadcast([P, P]), ident[:])
+        gain_row = sb("gain_row", [P, N], F32)
+        nc.scalar.copy(gain_row[:], spread[:])
 
         wp_raw = sb("wp_raw", [P, PASSES, 2 * N], U8)
         tab0 = sb("tab0", [P, T], I32)
@@ -107,8 +115,6 @@ def tile_list_stroke_circuit_evidence_kernel(
         we_raw = [sb("we_raw%d" % a, [P, PACK, H], F32) for a in range(PASSES)]
         for a in range(PASSES):
             nc.sync.dma_start(we_raw[a][:], we[512 * a : 512 * (a + 1), :].rearrange("(p j) r -> p j r", j=PACK))
-        with nc.allow_non_contiguous_dma(reason="one value a partition"):
-            nc.sync.dma_start(gains[1][:], gain_hbm[:, 3:4])
         wm_raw = sb("wm_raw", [P, N], I32)
         nc.sync.dma_start(wm_raw[:], wm_words[0].rearrange("p c i -> p (c i)").bitcast(I32))
 
@@ -134,19 +140,30 @@ def tile_list_stroke_circuit_evidence_kernel(
         for a in range(PASSES):
             for h in range(HALVES):
                 for t in range(PACK):
-                    nc.tensor.matmul_mx(
-                        acc[h][t][:],
-                        lhsT=wp[:, a, 2 * P * t : 2 * P * (t + 1)].bitcast(FP4X4),
-                        lhsT_scale=wp_sc[:, a, P * t : P * (t + 1)],
-                        rhs=v_words(a, h),
-                        rhs_scale=v_sc[:, a, HALF * h : HALF * (h + 1)],
-                        start=(a == 0),
-                        stop=(a == PASSES - 1),
-                    )
+                    if h == 0:
+                        nc.tensor.matmul_mx(
+                            acc[h][t][:],
+                            lhsT=wp[:, a, 2 * P * t : 2 * P * (t + 1)].bitcast(FP4X4),
+                            lhsT_scale=wp_sc[:, a, P * t : P * (t + 1)],
+                            rhs=v_words(a, h),
+                            rhs_scale=v_sc[:, a, 0:HALF],
+                            start=(a == 0),
+                            stop=(a == PASSES - 1),
+                        )
+                    else:
+                        nc.tensor.matmul_mx(
+                            acc[h][t][:],
+                            lhsT=(v0, v1)[a][h][:, P * t : P * (t + 1)].bitcast(FP8X4),
+                            lhsT_scale=v_sc[:, a, HALF + P * t : HALF + P * (t + 1)],
+                            rhs=wp[:, a, :].bitcast(FP4X4),
+                            rhs_scale=wp_sc[:, a, :],
+                            start=(a == 0),
+                            stop=(a == PASSES - 1),
+                        )
         prior = {}
-        for h, t in ((0, 0), (0, 1), (0, 2), (1, 0)):
-            prior[h, t] = sb("prior%d_%d" % (h, t), [P, HALF], F32)[:]
-            nc.scalar.activation(prior[h, t], acc[h][t][:], ACT.Copy, scale=gain_of(t))
+        for t in range(PACK):
+            prior[0, t] = sb("prior0_%d" % t, [P, HALF], F32)[:]
+            nc.scalar.activation(prior[0, t], acc[0][t][:], ACT.Copy, scale=gain_of(t))
 
         we_q = {}
         for a in range(PASSES):
@@ -155,8 +172,8 @@ def tile_list_stroke_circuit_evidence_kernel(
                 we_q[a, u] = (sb("we_c%d_%d" % (a, u), [P, 2 * P], U32), sb("we_s%d_%d" % (a, u), [P, 2 * P], U8))
             steps = [("v", 0, 0, P), ("v", 1, 0, P), ("q", 0, 0, 2 * P), ("q", 1, 0, 2 * P)]
             if a == 1:
-                steps = [("v", 0, 0, FIRST), ("s", 0, FIRST, P), ("v", 1, 0, SPLIT), ("q", 0, 0, P), ("q", 0, P, 2 * P)]
-                steps = steps + [("v", 1, SPLIT, P), ("q", 1, 0, 2 * P)]
+                steps = [("v", 0, 0, FIRST), ("s", 0, FIRST, P), ("s", 1, SPLIT, P), ("v", 1, 0, SPLIT), ("q", 0, 0, P)]
+                steps = steps + [("q", 0, P, 2 * P), ("q", 1, 0, 2 * P)]
             for kind, u, lo, hi in steps:
                 if kind == "q":
                     codes, scales = we_q[a, u]
@@ -171,13 +188,9 @@ def tile_list_stroke_circuit_evidence_kernel(
                         in_=we_raw[a][:].rearrange("p j (m t) -> p m j t", t=PACK)[:, lo:hi, :, 2 * u : 2 * u + 2],
                     )
 
-        for h in range(HALVES):
-            prior[h, 3] = sb("prior%d_3" % h, [P, HALF], F32)[:]
-            nc.scalar.activation(prior[h, 3], acc[h][3][:], ACT.Copy, scale=gain_of(3))
-        late = sb("prior1", [P, 2, HALF], F32, tag="we_raw1")
-        for t in range(1, PACK - 1):
-            prior[1, t] = late[:, t - 1, :]
-            nc.vector.tensor_scalar(prior[1, t], acc[1][t][:], gain_of(t), None, ALU.mult)
+        turned = sb("turned", [P, PACK, N], F32, tag="we_raw1")
+        for b in range(PACK):
+            nc.vector.tensor_tensor(turned[:, b, :], acc[1][b][:], gain_row[:], ALU.mult)
 
         wm = sb("wm", [P, N], I32, tag="we_g1_1")
         nc.gpsimd.tensor_copy(
@@ -185,12 +198,12 @@ def tile_list_stroke_circuit_evidence_kernel(
             in_=wm_raw[:].rearrange("p (c i t) -> p c t i", t=PACK, i=4),
         )
 
-        banks = ((0, 1, 2, 4), (5, 6, 3, 7))
+        banks = ((0, 1, 2, 3), (4, 5, 6, 7))
         acc = [[bank(banks[h][t]) for t in range(PACK)] for h in range(HALVES)]
         for h in range(HALVES):
             order = [(a, t) for a in range(PASSES) for t in range(PACK)]
             if h == 1:
-                order = [(a, t) for t in (2, 3, 0, 1) for a in (1, 0)]
+                order = [(a, t) for t in range(PACK) for a in (1, 0)]
             for a, t in order:
                 if True:
                     codes, scales = we_q[a, t // 2]
@@ -209,7 +222,7 @@ def tile_list_stroke_circuit_evidence_kernel(
         for h in range(HALVES):
             rows = sb("leaf_rows%d" % h, [P, PACK, HALF], BF16)
             all_rows.append(rows)
-            for t in ((0, 1, 2, 3), (2, 3, 0, 1))[h]:
+            for t in range(PACK):
                 nc.scalar.activation(rows[:, t, :], acc[h][t][:], ACT.Exp, bias=log_g[:, t : t + 1])
             grouped = sb("leaf_g%d" % h, [P, HALF, PACK], BF16, tag="y%d" % (1 - h))
             codes = sb("leaf_c%d" % h, [P, HALF], U32)
@@ -229,8 +242,14 @@ def tile_list_stroke_circuit_evidence_kernel(
         y = []
         for h in range(HALVES):
             y.append(sb("y%d" % h, [P, PACK, HALF], F32))
+            if h == 1:
+                for t in range(PACK):
+                    back = bank(PACK + t)
+                    for b in range(PACK):
+                        nc.tensor.transpose(back[:, P * b : P * (b + 1)], turned[:, b, P * t : P * (t + 1)], ident[:])
+                    prior[1, t] = back[:]
             for t in range(PACK):
-                mix = bank(banks[h][t])
+                mix = bank(t)
                 nc.tensor.matmul_mx(
                     mix[:],
                     lhsT=wm[:, P * t : P * (t + 1)].bitcast(FP8X4),
@@ -253,18 +272,27 @@ def tile_list_stroke_circuit_evidence_kernel(
         out_words = out_1[0].rearrange("p m t -> p (m t)").bitcast(I32)
         y_sc = sb("y_sc", [P, S], U8)
         y_g = [sb("y_g%d" % h, [P, HALF, PACK], BF16) for h in range(HALVES)]
-        for h, cut in enumerate((SHARE, QUARTER)):
-            interleave(nc.scalar.copy, y_g[h][:, 0:cut, :], y[h][:, :, 0:cut])
-            interleave(nc.vector.tensor_copy, y_g[h][:, cut:HALF, :], y[h][:, :, cut:HALF])
-        for name, h, lo, width in (("a", 0, 0, HALF), ("b", 1, QUARTER, QUARTER), ("c", 1, 0, QUARTER)):
-            codes = sb("y_c" + name, [P, width], I32)
-            cols = slice(HALF * h + lo, HALF * h + lo + width)
+        nc.gpsimd.tensor_scalar(
+            y_g[0][:, 0:SHARE, :], y[0][:, :, 0:SHARE].rearrange("p t c -> p c t"), 1.0, 0.0, ALU.mult, ALU.add
+        )
+        interleave(nc.scalar.copy, y_g[0][:, SHARE:HALF, :], y[0][:, :, SHARE:HALF])
+        interleave(nc.scalar.copy, y_g[1][:, 0:QUARTER, :], y[1][:, :, 0:QUARTER])
+        y_c = [sb("y_c%d" % h, [P, HALF], I32) for h in range(HALVES)]
+
+        def quantise_y(h, lo):
             nc.vector.quantize_mx(
-                out=codes[:].bitcast(FP8X4),
-                scales=y_sc[:, cols],
-                in_=y_g[h][:, lo : lo + width, :].rearrange("p j t -> p (j t)"),
+                out=y_c[h][:, lo : lo + QUARTER].bitcast(FP8X4),
+                scales=y_sc[:, HALF * h + lo : HALF * h + lo + QUARTER],
+                in_=y_g[h][:, lo : lo + QUARTER, :].rearrange("p j t -> p (j t)"),
             )
-            nc.sync.dma_start(out_words[:, cols], codes[:])
+
+        quantise_y(0, 0)
+        interleave(nc.vector.tensor_copy, y_g[1][:, QUARTER:HALF, :], y[1][:, :, QUARTER:HALF])
+        quantise_y(0, QUARTER)
+        nc.sync.dma_start(out_words[:, 0:HALF], y_c[0][:])
+        for lo in (QUARTER, 0):
+            quantise_y(1, lo)
+            nc.sync.dma_start(out_words[:, HALF + lo : HALF + lo + QUARTER], y_c[1][:, lo : lo + QUARTER])
         for q in range(4):
             (nc.sync if q % 2 == 0 else nc.scalar).dma_start(
                 out_2[0, 4 * q : 4 * q + 4, :].bitcast(I32), y_sc[32 * q : 32 * q + 4, :].bitcast(I32)

@@ -23,7 +23,7 @@ PASSES = 2
 HALF = 512
 HALVES = 2
 QUARTER = 256
-SHARE = 320
+SHARE = 256
 SPLIT = 64
 FIRST = 88
 LEAD = 2048
@@ -245,7 +245,7 @@ def tile_list_stroke_circuit_evidence_kernel(
             if h == 1:
                 for t in range(PACK):
                     back = bank(PACK + t)
-                    for b in range(PACK):
+                    for b in reversed(range(PACK)):
                         nc.tensor.transpose(back[:, P * b : P * (b + 1)], turned[:, b, P * t : P * (t + 1)], ident[:])
                     prior[1, t] = back[:]
             for t in range(PACK):
@@ -261,9 +261,13 @@ def tile_list_stroke_circuit_evidence_kernel(
                 )
                 log_mix = sb("log_mix%d_%d" % (h, t), [P, HALF], F32)
                 nc.scalar.activation(log_mix[:], mix[:], ACT.Ln)
-                nc.vector.scalar_tensor_tensor(
-                    y[h][:, t, :], log_mix[:], gain_of(t), prior[h, t], ALU.mult, ALU.add
-                )
+                parts = [slice(0, HALF)]
+                if (h, t) == (HALVES - 1, PACK - 1):
+                    parts = [slice(QUARTER, HALF), slice(0, QUARTER)]
+                for cols in parts:
+                    nc.vector.scalar_tensor_tensor(
+                        y[h][:, t, cols], log_mix[:, cols], gain_of(t), prior[h, t][:, cols], ALU.mult, ALU.add
+                    )
                 if t % 2 == 1:
                     nc.sync.dma_start(
                         out_rows[:, t - 1 : t + 1, HALF * h : HALF * (h + 1)], y[h][:, t - 1 : t + 1, :]
@@ -286,8 +290,8 @@ def tile_list_stroke_circuit_evidence_kernel(
                 in_=y_g[h][:, lo : lo + QUARTER, :].rearrange("p j t -> p (j t)"),
             )
 
-        quantise_y(0, 0)
         interleave(nc.vector.tensor_copy, y_g[1][:, QUARTER:HALF, :], y[1][:, :, QUARTER:HALF])
+        quantise_y(0, 0)
         quantise_y(0, QUARTER)
         nc.sync.dma_start(out_words[:, 0:HALF], y_c[0][:])
         for lo in (QUARTER, 0):

@@ -23,7 +23,8 @@ PASSES = 2
 HALF = 512
 HALVES = 2
 QUARTER = 256
-SHARE = 256
+SHARE = 224
+LATE = 192
 SPLIT = 64
 FIRST = 88
 LEAD = 2048
@@ -263,15 +264,14 @@ def tile_list_stroke_circuit_evidence_kernel(
                 nc.scalar.activation(log_mix[:], mix[:], ACT.Ln)
                 parts = [slice(0, HALF)]
                 if (h, t) == (HALVES - 1, PACK - 1):
-                    parts = [slice(QUARTER, HALF), slice(0, QUARTER)]
+                    parts = [slice(LATE, HALF), slice(0, LATE)]
                 for cols in parts:
                     nc.vector.scalar_tensor_tensor(
                         y[h][:, t, cols], log_mix[:, cols], gain_of(t), prior[h, t][:, cols], ALU.mult, ALU.add
                     )
-                if t % 2 == 1:
-                    nc.sync.dma_start(
-                        out_rows[:, t - 1 : t + 1, HALF * h : HALF * (h + 1)], y[h][:, t - 1 : t + 1, :]
-                    )
+                if (h, t) != (HALVES - 1, PACK - 2):
+                    first = t - 1 if (h, t) == (HALVES - 1, PACK - 1) else t
+                    nc.sync.dma_start(out_rows[:, first : t + 1, HALF * h : HALF * (h + 1)], y[h][:, first : t + 1, :])
 
         out_words = out_1[0].rearrange("p m t -> p (m t)").bitcast(I32)
         y_sc = sb("y_sc", [P, S], U8)
@@ -279,8 +279,9 @@ def tile_list_stroke_circuit_evidence_kernel(
         nc.gpsimd.tensor_scalar(
             y_g[0][:, 0:SHARE, :], y[0][:, :, 0:SHARE].rearrange("p t c -> p c t"), 1.0, 0.0, ALU.mult, ALU.add
         )
-        interleave(nc.scalar.copy, y_g[0][:, SHARE:HALF, :], y[0][:, :, SHARE:HALF])
-        interleave(nc.scalar.copy, y_g[1][:, 0:QUARTER, :], y[1][:, :, 0:QUARTER])
+        for cols in (slice(SHARE, QUARTER), slice(QUARTER, HALF)):
+            interleave(nc.scalar.copy, y_g[0][:, cols, :], y[0][:, :, cols])
+        interleave(nc.scalar.copy, y_g[1][:, 0:LATE, :], y[1][:, :, 0:LATE])
         y_c = [sb("y_c%d" % h, [P, HALF], I32) for h in range(HALVES)]
 
         def quantise_y(h, lo):
@@ -290,14 +291,14 @@ def tile_list_stroke_circuit_evidence_kernel(
                 in_=y_g[h][:, lo : lo + QUARTER, :].rearrange("p j t -> p (j t)"),
             )
 
-        interleave(nc.vector.tensor_copy, y_g[1][:, QUARTER:HALF, :], y[1][:, :, QUARTER:HALF])
+        interleave(nc.vector.tensor_copy, y_g[1][:, LATE:HALF, :], y[1][:, :, LATE:HALF])
         quantise_y(0, 0)
         quantise_y(0, QUARTER)
         nc.sync.dma_start(out_words[:, 0:HALF], y_c[0][:])
         for lo in (QUARTER, 0):
             quantise_y(1, lo)
             nc.sync.dma_start(out_words[:, HALF + lo : HALF + lo + QUARTER], y_c[1][:, lo : lo + QUARTER])
-        for q in range(4):
-            (nc.sync if q % 2 == 0 else nc.scalar).dma_start(
-                out_2[0, 4 * q : 4 * q + 4, :].bitcast(I32), y_sc[32 * q : 32 * q + 4, :].bitcast(I32)
+        for r in range(4):
+            (nc.sync if r % 2 == 0 else nc.scalar).dma_start(
+                out_2[0, r:16:4, :].bitcast(I32), y_sc[r:P:32, :].bitcast(I32)
             )

@@ -27,8 +27,6 @@ SHARE = 224
 LATE = 192
 SPLIT = 64
 FIRST = 88
-LEAD = 2048
-CUT = 1536
 ROWS = 96
 
 
@@ -57,16 +55,15 @@ def tile_list_stroke_circuit_evidence_kernel(
         nc.sync.dma_start(tab_sc[ROWS:P, :].bitcast(I32), tab_scales.bitcast(I32).rearrange("a i c -> i a c"))
         nc.sync.dma_start(offsets[:], offs)
         w_sc_raw = sb("w_sc_raw", [P, PASSES, N], U8)
-        nc.vector.memset(w_sc_raw[:].bitcast(I32), 0)
-        wm_sc = sb("wm_sc", [P, N], U8)
-        nc.vector.memset(wm_sc[:].bitcast(I32), 0)
+        nc.gpsimd.memset(w_sc_raw[:].bitcast(I32), 0)
         v_sc = sb("v_sc", [P, PASSES, S], U8)
         nc.vector.memset(v_sc[:].bitcast(I32), 0)
 
         g_sb = sb("g_sb", [P, PACK], F32)
-        nc.scalar.dma_start(g_sb[:], g.rearrange("(p t) -> p t", t=PACK))
+        nc.gpsimd.dma_start(g_sb[:], g.rearrange("(p t) -> p t", t=PACK))
         gain_sb = sb("gain_sb", [P, PACK], F32)
-        nc.scalar.dma_start(gain_sb[:], gain.rearrange("(p t) -> p t", t=PACK))
+        nc.gpsimd.dma_start(gain_sb[:], gain.rearrange("(p t) -> p t", t=PACK))
+        nc.gpsimd.dma_start(w_sc_raw[4:P:8, 0, :].bitcast(I32), wm_scales[0].bitcast(I32))
 
         def gain_of(t):
             return gain_sb[:, t : t + 1]
@@ -81,17 +78,14 @@ def tile_list_stroke_circuit_evidence_kernel(
 
         wp_raw = sb("wp_raw", [P, PASSES, 2 * N], U8)
         tab0 = sb("tab0", [P, T], I32)
-        tab1 = sb("tab1", [P, T], I32)
         tab0_hbm = tab_words[0].rearrange("p c i -> p (c i)").bitcast(I32)
-        nc.sync.dma_start(tab0[:, 0:LEAD], tab0_hbm[:, 0:LEAD])
         nc.sync.dma_start(wp_raw[:].bitcast(I32), wp_words.rearrange("a p c -> p a c").bitcast(I32))
         for q in range(4):
             nc.sync.dma_start(
                 w_sc_raw[32 * q : 32 * q + 4, :, :].bitcast(I32),
                 wp_scales[:, 4 * q : 4 * q + 4, :].rearrange("a r n -> r a n").bitcast(I32),
             )
-        nc.sync.dma_start(w_sc_raw[4:P:8, 0, :].bitcast(I32), wm_scales[0].bitcast(I32))
-        nc.sync.dma_start(tab0[:, LEAD:T], tab0_hbm[:, LEAD:T])
+        nc.sync.dma_start(tab0[:], tab0_hbm)
         tab1_hbm = tab_words[1].rearrange("p c i -> p (c i)").bitcast(I32)
 
         log_g = sb("log_g", [P, PACK], F32)
@@ -99,40 +93,44 @@ def tile_list_stroke_circuit_evidence_kernel(
         warm = sb("warm", [P, PACK], F32)
         nc.scalar.activation(warm[:], log_g[:], ACT.Exp)
 
+        picked_sc = sb("picked_sc", [P, S], U8)
+        nc.vector.tensor_copy(picked_sc[:], tab_sc[:].indirect(offsets[:]))
         wp = sb("wp", [P, PASSES, 2 * N], U8)
         nc.vector.tensor_copy(
             out=wp[:].bitcast(U16).rearrange("p a (t c i) -> p a c t i", t=PACK, i=8),
             in_=wp_raw[:].bitcast(U16).rearrange("p a (c i t) -> p a c t i", t=PACK, i=8),
         )
-        picked_sc = sb("picked_sc", [P, S], U8)
-        nc.vector.tensor_copy(picked_sc[:], tab_sc[:].indirect(offsets[:]))
-        nc.sync.dma_start(tab1[:, 0:CUT], tab1_hbm[:, 0:CUT])
         for q in range(4):
             nc.sync.dma_start(
                 v_sc[32 * q : 32 * q + 4, :, :].bitcast(I32),
                 picked_sc[ROWS + 8 * q : ROWS + 8 * (q + 1), :].bitcast(I32),
             )
-        nc.sync.dma_start(tab1[:, CUT:T], tab1_hbm[:, CUT:T])
-        we_raw = [sb("we_raw%d" % a, [P, PACK, H], F32) for a in range(PASSES)]
-        for a in range(PASSES):
-            nc.sync.dma_start(we_raw[a][:], we[512 * a : 512 * (a + 1), :].rearrange("(p j) r -> p j r", j=PACK))
-        wm_raw = sb("wm_raw", [P, N], I32)
-        nc.sync.dma_start(wm_raw[:], wm_words[0].rearrange("p c i -> p (c i)").bitcast(I32))
+        tab1 = sb("tab1", [P, T], I32, tag="tab_sc")
+        nc.sync.dma_start(tab1[:], tab1_hbm)
+        we_raw = [sb("we_raw0", [P, PACK, H], F32, tag="wp_raw")]
+        nc.sync.dma_start(we_raw[0][:], we[0:512, :].rearrange("(p j) r -> p j r", j=PACK))
 
         wp_sc = sb("wp_sc", [P, PASSES, N], U8)
         nc.vector.tensor_copy(
             out=wp_sc[:].rearrange("p a (t c i) -> p a c t i", t=PACK, i=16),
             in_=w_sc_raw[:].rearrange("p a (c i t) -> p a c t i", t=PACK, i=16),
         )
-        for r in range(4):
-            nc.sync.dma_start(wm_sc[r:P:32, :].bitcast(I32), wp_sc[8 * r + 4 : P : 32, 0, :].bitcast(I32))
         v0 = [sb("v0_%d" % h, [P, HALF], U32) for h in range(HALVES)]
         for h in range(HALVES):
             nc.vector.tensor_copy(v0[h][:], tab0[:].bitcast(U32).indirect(offsets[:, 32 * h : 32 * (h + 1)]))
+        we_raw.append(sb("we_raw1", [P, PACK, H], F32, tag="tab0"))
+        nc.sync.dma_start(we_raw[1][:], we[512:K, :].rearrange("(p j) r -> p j r", j=PACK))
 
         v1 = [sb("v1_%d" % h, [P, HALF], U32) for h in range(HALVES)]
         for h in range(HALVES):
             nc.vector.tensor_copy(v1[h][:], tab1[:].bitcast(U32).indirect(offsets[:, 32 * h : 32 * (h + 1)]))
+        wm_bytes = sb("wm_bytes", [P, 5 * N], U8, tag="tab_sc")
+        wm_raw = wm_bytes[:, 0 : 4 * N].bitcast(I32)
+        wm_sc = wm_bytes[:, 4 * N : 5 * N]
+        nc.gpsimd.memset(wm_sc.bitcast(I32), 0)
+        nc.sync.dma_start(wm_raw, wm_words[0].rearrange("p c i -> p (c i)").bitcast(I32))
+        for r in range(4):
+            nc.sync.dma_start(wm_sc[r:P:32, :].bitcast(I32), wp_sc[8 * r + 4 : P : 32, 0, :].bitcast(I32))
 
         def v_words(a, h):
             return (v0 if a == 0 else v1)[h][:].bitcast(FP8X4)
@@ -189,14 +187,14 @@ def tile_list_stroke_circuit_evidence_kernel(
                         in_=we_raw[a][:].rearrange("p j (m t) -> p m j t", t=PACK)[:, lo:hi, :, 2 * u : 2 * u + 2],
                     )
 
-        turned = sb("turned", [P, PACK, N], F32, tag="we_raw1")
+        turned = sb("turned", [P, PACK, N], F32, tag="tab0")
         for b in range(PACK):
             nc.vector.tensor_tensor(turned[:, b, :], acc[1][b][:], gain_row[:], ALU.mult)
 
         wm = sb("wm", [P, N], I32, tag="we_g1_1")
         nc.gpsimd.tensor_copy(
             out=wm[:].rearrange("p (t c i) -> p c t i", t=PACK, i=4),
-            in_=wm_raw[:].rearrange("p (c i t) -> p c t i", t=PACK, i=4),
+            in_=wm_raw.rearrange("p (c i t) -> p c t i", t=PACK, i=4),
         )
 
         banks = ((0, 1, 2, 3), (4, 5, 6, 7))
@@ -206,18 +204,17 @@ def tile_list_stroke_circuit_evidence_kernel(
             if h == 1:
                 order = [(a, t) for t in range(PACK) for a in (1, 0)]
             for a, t in order:
-                if True:
-                    codes, scales = we_q[a, t // 2]
-                    cols = slice(P * (t % 2), P * (t % 2 + 1))
-                    nc.tensor.matmul_mx(
-                        acc[h][t][:],
-                        lhsT=codes[:, cols].bitcast(FP8X4),
-                        lhsT_scale=scales[:, cols],
-                        rhs=v_words(a, h),
-                        rhs_scale=v_sc[:, a, HALF * h : HALF * (h + 1)],
-                        start=(a == h),
-                        stop=(a != h),
-                    )
+                codes, scales = we_q[a, t // 2]
+                cols = slice(P * (t % 2), P * (t % 2 + 1))
+                nc.tensor.matmul_mx(
+                    acc[h][t][:],
+                    lhsT=codes[:, cols].bitcast(FP8X4),
+                    lhsT_scale=scales[:, cols],
+                    rhs=v_words(a, h),
+                    rhs_scale=v_sc[:, a, HALF * h : HALF * (h + 1)],
+                    start=(a == h),
+                    stop=(a != h),
+                )
         leaf_q = []
         all_rows = []
         for h in range(HALVES):

@@ -124,13 +124,8 @@ def tile_list_stroke_circuit_evidence_kernel(
         v1 = [sb("v1_%d" % h, [P, HALF], U32) for h in range(HALVES)]
         for h in range(HALVES):
             nc.vector.tensor_copy(v1[h][:], tab1[:].bitcast(U32).indirect(offsets[:, 32 * h : 32 * (h + 1)]))
-        wm_bytes = sb("wm_bytes", [P, 5 * N], U8, tag="tab_sc")
-        wm_raw = wm_bytes[:, 0 : 4 * N].bitcast(I32)
-        wm_sc = wm_bytes[:, 4 * N : 5 * N]
-        nc.gpsimd.memset(wm_sc.bitcast(I32), 0)
-        nc.sync.dma_start(wm_raw, wm_words[0].rearrange("p c i -> p (c i)").bitcast(I32))
-        for r in range(4):
-            nc.sync.dma_start(wm_sc[r:P:32, :].bitcast(I32), wp_sc[8 * r + 4 : P : 32, 0, :].bitcast(I32))
+        wm_raw = sb("wm_raw", [P, N], I32, tag="tab_sc")
+        nc.sync.dma_start(wm_raw[:], wm_words[0].rearrange("p c i -> p (c i)").bitcast(I32))
 
         def v_words(a, h):
             return (v0 if a == 0 else v1)[h][:].bitcast(FP8X4)
@@ -159,6 +154,9 @@ def tile_list_stroke_circuit_evidence_kernel(
                             start=(a == 0),
                             stop=(a == PASSES - 1),
                         )
+        for r in range(4):
+            nc.sync.dma_start(wp_sc[4 + r : P : 32, 1, :].bitcast(I32), wp_sc[8 * r + 4 : P : 32, 0, :].bitcast(I32))
+        wm_sc = wp_sc[4:P, 1, :]
         prior = {}
         for t in range(PACK):
             prior[0, t] = sb("prior0_%d" % t, [P, HALF], F32)[:]
@@ -194,7 +192,7 @@ def tile_list_stroke_circuit_evidence_kernel(
         wm = sb("wm", [P, N], I32, tag="we_g1_1")
         nc.gpsimd.tensor_copy(
             out=wm[:].rearrange("p (t c i) -> p c t i", t=PACK, i=4),
-            in_=wm_raw.rearrange("p (c i t) -> p c t i", t=PACK, i=4),
+            in_=wm_raw[:].rearrange("p (c i t) -> p c t i", t=PACK, i=4),
         )
 
         banks = ((0, 1, 2, 3), (4, 5, 6, 7))

from contextlib import ExitStack

import concourse.mybir as mybir
from concourse.masks import make_identity

K, T, S, H, N = 1024, 4096, 1024, 512, 512
FLOPS = 2 * S * (K * H + H * N + K * N)

F32 = mybir.dt.float32
BF16 = mybir.dt.bfloat16
I32 = mybir.dt.int32
U32 = mybir.dt.uint32
U16 = mybir.dt.uint16
U8 = mybir.dt.uint8
FP8X4 = mybir.dt.float8_e4m3fn_x4
FP4X4 = mybir.dt.float4_e2m1fn_x4
ACT = mybir.ActivationFunctionType
ALU = mybir.AluOpType

P = 128
PACK = 4
PASSES = 2
HALF = 512
HALVES = 2
QUARTER = 256
SHARE = 224
LATE = 192
SPLIT = 64
FIRST = 88
ROWS = 96


def interleave(copy, dst, src):
    copy(out=dst.rearrange("p (c i) t -> p c t i", i=4), in_=src.rearrange("p t (c i) -> p c t i", i=4))


def tile_list_stroke_circuit_evidence_kernel(
    tc, tab_words, tab_scales, offs, we, g, wm_words, wm_scales, wp_words, wp_scales, gain, out_0, out_1, out_2
):
    nc = tc.nc
    with ExitStack() as ctx:
        keep = ctx.enter_context(tc.tile_pool(name="keep", bufs=1))
        psum = ctx.enter_context(tc.psum_pool(name="psum", bufs=1))

        def sb(name, shape, dtype, tag=None):
            return keep.tile(shape, dtype, name=name, tag=tag or name, align_bytes=64)

        def bank(b):
            return psum.tile([P, HALF], F32, name="bank%d" % b)

        offsets = keep.tile([P, S // 16], U16, name="offsets")

        tab_sc = sb("tab_sc", [P, T], U8)
        nc.vector.memset(tab_sc[0:ROWS, :].bitcast(I32), 0)
        nc.sync.dma_start(tab_sc[ROWS:P, :].bitcast(I32), tab_scales.bitcast(I32).rearrange("a i c -> i a c"))
        nc.sync.dma_start(offsets[:], offs)
        w_sc_raw = sb("w_sc_raw", [P, PASSES, N], U8)
        nc.gpsimd.memset(w_sc_raw[:].bitcast(I32), 0)
        v_sc = sb("v_sc", [P, PASSES, S], U8)
        nc.vector.memset(v_sc[:].bitcast(I32), 0)

        g_sb = sb("g_sb", [P, PACK], F32)
        nc.gpsimd.dma_start(g_sb[:], g.rearrange("(p t) -> p t", t=PACK))
        gain_sb = sb("gain_sb", [P, PACK], F32)
        nc.gpsimd.dma_start(gain_sb[:], gain.rearrange("(p t) -> p t", t=PACK))
        nc.gpsimd.dma_start(w_sc_raw[4:P:8, 0, :].bitcast(I32), wm_scales[0].bitcast(I32))

        def gain_of(t):
            return gain_sb[:, t : t + 1]

        ident = sb("ident", [P, P], F32)
        make_identity(nc, ident[:])
        spread = bank(7)
        for t in range(PACK):
            nc.tensor.transpose(spread[:, P * t : P * (t + 1)], gain_of(t).to_broadcast([P, P]), ident[:])
        gain_row = sb("gain_row", [P, N], F32)
        nc.scalar.copy(gain_row[:], spread[:])

        wp_raw = sb("wp_raw", [P, PASSES, 2 * N], U8)
        tab0 = sb("tab0", [P, T], I32)
        tab0_hbm = tab_words[0].rearrange("p c i -> p (c i)").bitcast(I32)
        nc.sync.dma_start(wp_raw[:].bitcast(I32), wp_words.rearrange("a p c -> p a c").bitcast(I32))
        for q in range(4):
            nc.sync.dma_start(
                w_sc_raw[32 * q : 32 * q + 4, :, :].bitcast(I32),
                wp_scales[:, 4 * q : 4 * q + 4, :].rearrange("a r n -> r a n").bitcast(I32),
            )
        nc.sync.dma_start(tab0[:], tab0_hbm)
        tab1_hbm = tab_words[1].rearrange("p c i -> p (c i)").bitcast(I32)

        log_g = sb("log_g", [P, PACK], F32)
        nc.scalar.activation(log_g[:], g_sb[:], ACT.Ln)
        warm = sb("warm", [P, PACK], F32)
        nc.scalar.activation(warm[:], log_g[:], ACT.Exp)

        picked_sc = sb("picked_sc", [P, S], U8)
        nc.vector.tensor_copy(picked_sc[:], tab_sc[:].indirect(offsets[:]))
        wp = sb("wp", [P, PASSES, 2 * N], U8)
        nc.vector.tensor_copy(
            out=wp[:].bitcast(U16).rearrange("p a (t c i) -> p a c t i", t=PACK, i=8),
            in_=wp_raw[:].bitcast(U16).rearrange("p a (c i t) -> p a c t i", t=PACK, i=8),
        )
        for q in range(4):
            nc.sync.dma_start(
                v_sc[32 * q : 32 * q + 4, :, :].bitcast(I32),
                picked_sc[ROWS + 8 * q : ROWS + 8 * (q + 1), :].bitcast(I32),
            )
        tab1 = sb("tab1", [P, T], I32, tag="tab_sc")
        nc.sync.dma_start(tab1[:], tab1_hbm)
        we_raw = [sb("we_raw0", [P, PACK, H], F32, tag="wp_raw")]
        nc.sync.dma_start(we_raw[0][:], we[0:512, :].rearrange("(p j) r -> p j r", j=PACK))

        wp_sc = sb("wp_sc", [P, PASSES, N], U8)
        nc.vector.tensor_copy(
            out=wp_sc[:].rearrange("p a (t c i) -> p a c t i", t=PACK, i=16),
            in_=w_sc_raw[:].rearrange("p a (c i t) -> p a c t i", t=PACK, i=16),
        )
        v0 = [sb("v0_%d" % h, [P, HALF], U32) for h in range(HALVES)]
        for h in range(HALVES):
            nc.vector.tensor_copy(v0[h][:], tab0[:].bitcast(U32).indirect(offsets[:, 32 * h : 32 * (h + 1)]))
        we_raw.append(sb("we_raw1", [P, PACK, H], F32, tag="tab0"))
        nc.sync.dma_start(we_raw[1][:], we[512:K, :].rearrange("(p j) r -> p j r", j=PACK))

        v1 = [sb("v1_%d" % h, [P, HALF], U32) for h in range(HALVES)]
        for h in range(HALVES):
            nc.vector.tensor_copy(v1[h][:], tab1[:].bitcast(U32).indirect(offsets[:, 32 * h : 32 * (h + 1)]))
        wm_raw = sb("wm_raw", [P, N], I32, tag="tab_sc")
        nc.sync.dma_start(wm_raw[:], wm_words[0].rearrange("p c i -> p (c i)").bitcast(I32))

        def v_words(a, h):
            return (v0 if a == 0 else v1)[h][:].bitcast(FP8X4)

        acc = [[bank(PACK * h + t) for t in range(PACK)] for h in range(HALVES)]
        for a in range(PASSES):
            for h in range(HALVES):
                for t in range(PACK):
                    if h == 0:
                        nc.tensor.matmul_mx(
                            acc[h][t][:],
                            lhsT=wp[:, a, 2 * P * t : 2 * P * (t + 1)].bitcast(FP4X4),
                            lhsT_scale=wp_sc[:, a, P * t : P * (t + 1)],
                            rhs=v_words(a, h),
                            rhs_scale=v_sc[:, a, 0:HALF],
                            start=(a == 0),
                            stop=(a == PASSES - 1),
                        )
                    else:
                        nc.tensor.matmul_mx(
                            acc[h][t][:],
                            lhsT=(v0, v1)[a][h][:, P * t : P * (t + 1)].bitcast(FP8X4),
                            lhsT_scale=v_sc[:, a, HALF + P * t : HALF + P * (t + 1)],
                            rhs=wp[:, a, :].bitcast(FP4X4),
                            rhs_scale=wp_sc[:, a, :],
                            start=(a == 0),
                            stop=(a == PASSES - 1),
                        )
        for r in range(4):
            nc.sync.dma_start(wp_sc[4 + r : P : 32, 1, :].bitcast(I32), wp_sc[8 * r + 4 : P : 32, 0, :].bitcast(I32))
        wm_sc = wp_sc[4:P, 1, :]
        prior = {}
        for t in range(PACK):
            prior[0, t] = sb("prior0_%d" % t, [P, HALF], F32)[:]
            nc.scalar.activation(prior[0, t], acc[0][t][:], ACT.Copy, scale=gain_of(t))

        we_q = {}
        for a in range(PASSES):
            pairs = [sb("we_g%d_%d" % (a, u), [P, 2, P, PACK], BF16) for u in range(2)]
            for u in range(2):
                we_q[a, u] = (sb("we_c%d_%d" % (a, u), [P, 2 * P], U32), sb("we_s%d_%d" % (a, u), [P, 2 * P], U8))
            steps = [("v", 0, 0, P), ("v", 1, 0, P), ("q", 0, 0, 2 * P), ("q", 1, 0, 2 * P)]
            if a == 1:
                steps = [("v", 0, 0, FIRST), ("s", 0, FIRST, P), ("s", 1, SPLIT, P), ("v", 1, 0, SPLIT), ("q", 0, 0, P)]
                steps = steps + [("q", 0, P, 2 * P), ("q", 1, 0, 2 * P)]
            for kind, u, lo, hi in steps:
                if kind == "q":
                    codes, scales = we_q[a, u]
                    nc.vector.quantize_mx(
                        out=codes[:, lo:hi].bitcast(FP8X4),
                        scales=scales[:, lo:hi],
                        in_=pairs[u][:].rearrange("p t m j -> p (t m j)")[:, PACK * lo : PACK * hi],
                    )
                else:
                    (nc.scalar.copy if kind == "s" else nc.vector.tensor_copy)(
                        out=pairs[u][:].rearrange("p t m j -> p m j t")[:, lo:hi],
                        in_=we_raw[a][:].rearrange("p j (m t) -> p m j t", t=PACK)[:, lo:hi, :, 2 * u : 2 * u + 2],
                    )

        turned = sb("turned", [P, PACK, N], F32, tag="tab0")
        for b in range(PACK):
            nc.vector.tensor_tensor(turned[:, b, :], acc[1][b][:], gain_row[:], ALU.mult)

        wm = sb("wm", [P, N], I32, tag="we_g1_1")
        nc.gpsimd.tensor_copy(
            out=wm[:].rearrange("p (t c i) -> p c t i", t=PACK, i=4),
            in_=wm_raw[:].rearrange("p (c i t) -> p c t i", t=PACK, i=4),
        )

        banks = ((0, 1, 2, 3), (4, 5, 6, 7))
        acc = [[bank(banks[h][t]) for t in range(PACK)] for h in range(HALVES)]
        for h in range(HALVES):
            order = [(a, t) for a in range(PASSES) for t in range(PACK)]
            if h == 1:
                order = [(a, t) for t in range(PACK) for a in (1, 0)]
            for a, t in order:
                codes, scales = we_q[a, t // 2]
                cols = slice(P * (t % 2), P * (t % 2 + 1))
                nc.tensor.matmul_mx(
                    acc[h][t][:],
                    lhsT=codes[:, cols].bitcast(FP8X4),
                    lhsT_scale=scales[:, cols],
                    rhs=v_words(a, h),
                    rhs_scale=v_sc[:, a, HALF * h : HALF * (h + 1)],
                    start=(a == h),
                    stop=(a != h),
                )
        leaf_q = []
        all_rows = []
        for h in range(HALVES):
            rows = sb("leaf_rows%d" % h, [P, PACK, HALF], BF16)
            all_rows.append(rows)
            for t in range(PACK):
                nc.scalar.activation(rows[:, t, :], acc[h][t][:], ACT.Exp, bias=log_g[:, t : t + 1])
            grouped = sb("leaf_g%d" % h, [P, HALF, PACK], BF16, tag="y%d" % (1 - h))
            codes = sb("leaf_c%d" % h, [P, HALF], U32)
            scales = sb("leaf_s%d" % h, [P, HALF], U8)
            quarters = [slice(0, QUARTER), slice(QUARTER, HALF)]
            for cols in quarters:
                interleave(nc.vector.tensor_copy, grouped[:, cols, :], rows[:, :, cols])
            for cols in quarters:
                nc.vector.quantize_mx(
                    out=codes[:, cols].bitcast(FP8X4),
                    scales=scales[:, cols],
                    in_=grouped[:, cols, :].rearrange("p j t -> p (j t)"),
                )
            leaf_q.append((codes, scales))

        out_rows = out_0.rearrange("(p t) j -> p t j", t=PACK)
        y = []
        for h in range(HALVES):
            y.append(sb("y%d" % h, [P, PACK, HALF], F32))
            if h == 1:
                for t in range(PACK):
                    back = bank(PACK + t)
                    for b in reversed(range(PACK)):
                        nc.tensor.transpose(back[:, P * b : P * (b + 1)], turned[:, b, P * t : P * (t + 1)], ident[:])
                    prior[1, t] = back[:]
            for t in range(PACK):
                mix = bank(t)
                nc.tensor.matmul_mx(
                    mix[:],
                    lhsT=wm[:, P * t : P * (t + 1)].bitcast(FP8X4),
                    lhsT_scale=wm_sc[:, P * t : P * (t + 1)],
                    rhs=leaf_q[h][0][:].bitcast(FP8X4),
                    rhs_scale=leaf_q[h][1][:],
                    start=True,
                    stop=True,
                )
                log_mix = sb("log_mix%d_%d" % (h, t), [P, HALF], F32)
                nc.scalar.activation(log_mix[:], mix[:], ACT.Ln)
                parts = [slice(0, HALF)]
                if (h, t) == (HALVES - 1, PACK - 1):
                    parts = [slice(LATE, HALF), slice(0, LATE)]
                for cols in parts:
                    nc.vector.scalar_tensor_tensor(
                        y[h][:, t, cols], log_mix[:, cols], gain_of(t), prior[h, t][:, cols], ALU.mult, ALU.add
                    )
                if (h, t) != (HALVES - 1, PACK - 2):
                    first = t - 1 if (h, t) == (HALVES - 1, PACK - 1) else t
                    nc.sync.dma_start(out_rows[:, first : t + 1, HALF * h : HALF * (h + 1)], y[h][:, first : t + 1, :])

        out_words = out_1[0].rearrange("p m t -> p (m t)").bitcast(I32)
        y_sc = sb("y_sc", [P, S], U8)
        y_g = [sb("y_g%d" % h, [P, HALF, PACK], BF16) for h in range(HALVES)]
        nc.gpsimd.tensor_scalar(
            y_g[0][:, 0:SHARE, :], y[0][:, :, 0:SHARE].rearrange("p t c -> p c t"), 1.0, 0.0, ALU.mult, ALU.add
        )
        for cols in (slice(SHARE, QUARTER), slice(QUARTER, HALF)):
            interleave(nc.scalar.copy, y_g[0][:, cols, :], y[0][:, :, cols])
        interleave(nc.scalar.copy, y_g[1][:, 0:LATE, :], y[1][:, :, 0:LATE])
        y_c = [sb("y_c%d" % h, [P, HALF], I32) for h in range(HALVES)]

        def quantise_y(h, lo):
            nc.vector.quantize_mx(
                out=y_c[h][:, lo : lo + QUARTER].bitcast(FP8X4),
                scales=y_sc[:, HALF * h + lo : HALF * h + lo + QUARTER],
                in_=y_g[h][:, lo : lo + QUARTER, :].rearrange("p j t -> p (j t)"),
            )

        interleave(nc.vector.tensor_copy, y_g[1][:, LATE:HALF, :], y[1][:, :, LATE:HALF])
        quantise_y(0, 0)
        quantise_y(0, QUARTER)
        nc.sync.dma_start(out_words[:, 0:HALF], y_c[0][:])
        for lo in (QUARTER, 0):
            quantise_y(1, lo)
            nc.sync.dma_start(out_words[:, HALF + lo : HALF + lo + QUARTER], y_c[1][:, lo : lo + QUARTER])
        for r in range(4):
            (nc.sync if r % 2 == 0 else nc.scalar).dma_start(
                out_2[0, r:16:4, :].bitcast(I32), y_sc[r:P:32, :].bitcast(I32)
            )
